import numpy as np
import ml_dtypes


def mxq(x, axis, fmt="e4m3"):
    dtype, down = {"e4m3": (ml_dtypes.float8_e4m3fn, 7), "e5m2": (ml_dtypes.float8_e5m2, 14)}[fmt]
    v = np.moveaxis(np.asarray(x, np.float32).astype(ml_dtypes.bfloat16).astype(np.float64), axis, -1)
    blocks = v.reshape(v.shape[:-1] + (-1, 32))
    amax = np.abs(blocks).max(-1, keepdims=True)
    byte = np.maximum(np.where(amax > 0, np.frexp(amax)[1] - 1 + 127, 0) - down, 1)
    scale = np.exp2(byte - 127.0)
    codes = (blocks / scale).astype(np.float32).astype(dtype).astype(np.float64)
    return np.moveaxis((codes * scale).reshape(v.shape), -1, axis)


WIDE = False


def mx_kscale(k):
    if not WIDE:
        return np.ones(k)
    levels = np.array([10, -10, 5, -5, 0])
    if k % 512:
        return np.exp2(np.random.permutation(np.resize(levels, k // 32))).repeat(32)
    a = np.empty((k // 512, 16))
    for p in range(k // 512):
        a[p, :8] = np.random.permutation(np.resize(levels, 8))
        for g in range(8):
            far = levels[np.abs(levels - a[p, g]) >= 10]
            a[p, g + 8] = far[np.random.randint(len(far))]
    return np.exp2(a.ravel()).repeat(32)


BF16 = ml_dtypes.bfloat16


def bf(x):
    return np.asarray(x, np.float32).astype(BF16)


def f64(x):
    return np.asarray(x).astype(np.float64)


E2M1 = np.array([0.0, 0.5, 1.0, 1.5, 2.0, 3.0, 4.0, 6.0, -0.0, -0.5, -1.0, -1.5, -2.0, -3.0, -4.0, -6.0])


def pack_weight(w, fmt):
    k, n = w.shape
    w = f64(bf(w)).reshape(k // 32, 32, n)
    amax = np.abs(w).max(1)
    if fmt == "e4m3":
        byte = np.frexp(amax)[1] - 1 + 127 - 7
    else:
        mant, ex = np.frexp(amax / 6.0)
        byte = np.where(mant > 0.5, ex, ex - 1) + 127
    byte = np.clip(np.where(amax > 0, byte, 1), 1, 254)
    scaled = (w * np.exp2(127.0 - byte)[:, None, :]).reshape(k, n).astype(np.float32)
    by_word = np.ascontiguousarray(scaled.reshape(k // 512, 128, 4, n).transpose(0, 1, 3, 2))
    if fmt == "e4m3":
        words = by_word.astype(ml_dtypes.float8_e4m3fn).view(np.uint8)
    else:
        c = by_word.astype(ml_dtypes.float4_e2m1fn).view(np.uint8) & 0xF
        words = c[..., 0::2] | (c[..., 1::2] << 4)
    return np.ascontiguousarray(words), np.ascontiguousarray(byte.astype(np.uint8).reshape(k // 512, 16, n))


def unpack_weight(words, scales, fmt):
    g, p, n, _ = words.shape
    if fmt == "e4m3":
        vals = np.ascontiguousarray(words).view(ml_dtypes.float8_e4m3fn).astype(np.float64)
    else:
        nib = np.empty((g, p, n, 4), np.uint8)
        nib[..., 0::2] = words & 0xF
        nib[..., 1::2] = words >> 4
        vals = E2M1[nib]
    vals = vals * np.repeat(np.exp2(scales.astype(np.float64) - 127.0), 8, axis=1)[..., None]
    return vals.transpose(0, 1, 3, 2).reshape(g * 512, n)
def pack4(w):
    words, scales = pack_weight(w, "e2m1")
    return words.reshape(words.shape[0], 128, -1), scales


def unpack4(words, scales):
    return unpack_weight(words.reshape(words.shape[0], 128, -1, 2), scales, "e2m1")


def planes(Y):
    n, m = Y.shape
    b = f64(bf(Y)).reshape(n // 32, 32, m)
    amax = np.abs(b).max(1)
    byte = np.clip(np.where(amax > 0, np.frexp(amax)[1] - 1 + 127 - 7, 1), 1, 254)
    codes = (b * np.exp2(127.0 - byte)[:, None, :]).reshape(n, m).astype(np.float32).astype(ml_dtypes.float8_e4m3fn).view(np.uint8)
    words = codes.reshape(n // 512, 128, 4, m).transpose(0, 1, 3, 2)
    return np.ascontiguousarray(words), np.ascontiguousarray(byte.astype(np.uint8).reshape(n // 512, 16, m))


N, P, E, R = 1024, 1024, 1024, 8
O = P // R


def fourth_power(v):
    sq = v * v
    return sq * sq


def setup_inputs():
    s, t = mx_kscale(P), mx_kscale(E)
    x = bf(np.random.standard_normal((N, P)) * s)
    dlt_words, dlt_scales = pack4(np.random.standard_normal((P, E)) * (0.25 / np.sqrt(P)) / s[:, None])
    f0 = bf(np.random.uniform(0.8, 1.2, E))
    cap = bf(np.random.uniform(0.9, 1.3, E))
    t0 = bf(np.random.uniform(4.0, 8.0, E) * t)
    perc_words, perc_scales = pack4(np.random.standard_normal((E, P)) / np.sqrt(E) / t[:, None])
    c0 = bf(np.random.standard_normal(P) * 0.5)
    return {
        "x": x,
        "dlt_words": dlt_words,
        "dlt_scales": dlt_scales,
        "f0": f0,
        "cap": cap,
        "t0": t0,
        "perc_words": perc_words,
        "perc_scales": perc_scales,
        "c0": c0,
    }


def core(x, dlt_words, dlt_scales, f0, cap, t0, perc_words, perc_scales, c0):
    f0 = f64(f0)
    cap = f64(cap)
    f = f0 + (mxq(f64(x), 1, "e4m3") @ unpack4(dlt_words, dlt_scales))
    e = 0.15 * f64(t0) * (fourth_power(f / cap) - fourth_power(f0 / cap))
    c = f64(c0) + (mxq(e, 1, "e4m3") @ unpack4(perc_words, perc_scales))
    c_od = np.reshape(c, (c.shape[0], O, R))
    z = -c_od
    w = np.exp(z - z.max(axis=-1, keepdims=True))
    s = w / w.sum(axis=-1, keepdims=True)
    y = R * s - 1.0
    return np.reshape(y, c.shape)


def reference(x, dlt_words, dlt_scales, f0, cap, t0, perc_words, perc_scales, c0):
    R_out = core(x, dlt_words, dlt_scales, f0, cap, t0, perc_words, perc_scales, c0)
    words, scales = planes(R_out)
    return R_out, words, scales

@@ -1,0 +1,588 @@
+from contextlib import ExitStack
+
+import concourse.mybir as mybir
+from concourse.masks import make_identity
+
+F32 = mybir.dt.float32
+BF16 = mybir.dt.bfloat16
+U32 = mybir.dt.uint32
+I32 = mybir.dt.int32
+U8 = mybir.dt.uint8
+FP8X4 = mybir.dt.float8_e4m3fn_x4
+FP4X4 = mybir.dt.float4_e2m1fn_x4
+ALU = mybir.AluOpType
+ACT = mybir.ActivationFunctionType
+
+N = 1024
+D = 1024
+R = 8
+P = 128
+HALF = 512
+
+FLOPS = 2 * 2 * N * D * D
+
+
+def tile_bprexcessdelaylogitroutesplit_x2_kernel(
+    tc, x, dlt_words, dlt_scales, f0, cap, t0, perc_words, perc_scales, c0, out_0, out_1, out_2
+):
+    nc = tc.nc
+    with ExitStack() as ctx:
+        keep = ctx.enter_context(tc.tile_pool(name="keep", bufs=1))
+        two = ctx.enter_context(tc.tile_pool(name="two", bufs=2))
+        five = ctx.enter_context(tc.tile_pool(name="five", bufs=5))
+        three = ctx.enter_context(tc.tile_pool(name="three", bufs=3))
+        turn = ctx.enter_context(tc.psum_pool(name="turn", bufs=3))
+        mm = ctx.enter_context(tc.psum_pool(name="mm", bufs=3))
+        small = ctx.enter_context(tc.psum_pool(name="small", bufs=2))
+
+        x_rows = x.rearrange("(g m t) k -> g m t k", g=2, t=4)
+        x_sb = [keep.tile([P, 4, D], BF16, name="x_sb%d" % g, align_bytes=64) for g in range(2)]
+        raw, raw_s, vec = {}, {}, {}
+        for key in ("dlt", "perc"):
+            raw[key] = keep.tile([P, 2, 2 * D], U8, name="raw_" + key, align_bytes=64)
+            raw_s[key] = keep.tile([P, 2, D], U8, name="raws_" + key, align_bytes=64)
+
+        def load_words(key, src, h):
+            cols = slice(256 * h, 256 * (h + 1))
+            nc.sync.dma_start(
+                out=raw[key][:].rearrange("p g b -> p (g b)").bitcast(I32).rearrange("p (g w) -> p g w", g=2)[:, :, cols],
+                in_=src.bitcast(I32).rearrange("g p w -> p g w")[:, :, cols],
+            )
+
+        def load_scales(key, src, eng):
+            for q in range(4):
+                eng.dma_start(
+                    out=raw_s[key][32 * q : 32 * q + 4, :, :].bitcast(I32),
+                    in_=src[:, 4 * q : 4 * q + 4, :].bitcast(I32).rearrange("g q w -> q g w"),
+                )
+
+        nc.vector.memset(raw_s["dlt"][:].rearrange("p g n -> p (g n)").bitcast(I32), 0)
+        nc.vector.memset(raw_s["perc"][:].rearrange("p g n -> p (g n)").bitcast(I32), 0)
+        load_scales("dlt", dlt_scales, nc.scalar)
+        load_words("dlt", dlt_words, 0)
+        load_words("dlt", dlt_words, 1)
+        load_scales("perc", perc_scales, nc.gpsimd)
+        for t in range(4):
+            nc.sync.dma_start(out=x_sb[0][:, t, :], in_=x_rows[0, :, t, :])
+        load_words("perc", perc_words, 0)
+        load_words("perc", perc_words, 1)
+        for key, src in (("f0", f0), ("cap", cap), ("t0", t0)):
+            vec[key] = keep.tile([P, 2, 4], BF16, name="v_" + key)
+            nc.gpsimd.dma_start(out=vec[key][:], in_=src.rearrange("(h p t) -> p h t", h=2, t=4))
+        c0_bf = keep.tile([P, R], BF16)
+        nc.gpsimd.dma_start(out=c0_bf[:], in_=c0.rearrange("(o r) -> o r", r=R))
+        for t in range(4):
+            nc.sync.dma_start(out=x_sb[1][:, t, :], in_=x_rows[1, :, t, :])
+
+        ident = keep.tile([P, P], F32)
+        make_identity(nc, ident[:])
+
+        dw = keep.tile([P, 2, 2 * D], U8, align_bytes=64)
+        ds = keep.tile([P, 2, D], U8, align_bytes=64)
+        pw = keep.tile([P, 2, 2 * D], U8, align_bytes=64)
+        psc = keep.tile([P, 2, D], U8, align_bytes=64)
+
+        def perm_dlt(h):
+            for g in range(2):
+                nc.vector.tensor_copy(
+                    out=dw[:, g, 1024 * h : 1024 * (h + 1)].rearrange("p (t m b) -> p t m b", t=4, b=2),
+                    in_=raw["dlt"][:, g, 1024 * h : 1024 * (h + 1)].rearrange("p (m t b) -> p t m b", t=4, b=2),
+                )
+            for g in range(2):
+                nc.vector.tensor_copy(
+                    out=ds[:, g, HALF * h : HALF * (h + 1)].rearrange("p (t m) -> p t m", t=4),
+                    in_=raw_s["dlt"][:, g, HALF * h : HALF * (h + 1)].rearrange("p (m t) -> p t m", t=4),
+                )
+
+        def perm_perc_words(g):
+            nc.vector.tensor_copy(
+                out=pw[:, g, :].rearrange("p (r o b) -> p r o b", r=R, b=2),
+                in_=raw["perc"][:, g, :].rearrange("p (o r b) -> p r o b", r=R, b=2),
+            )
+
+        def perm_perc_scales(g):
+            nc.vector.tensor_copy(
+                out=psc[:, g, :].rearrange("p (r o) -> p r o", r=R),
+                in_=raw_s["perc"][:, g, :].rearrange("p (o r) -> p r o", r=R),
+            )
+
+        def flat(tile):
+            return tile[:].rearrange("p h t -> p (h t)")
+
+        inv_cap = keep.tile([P, 8], F32)
+        base = keep.tile([P, 8], F32)
+        base2 = keep.tile([P, 8], F32)
+        base4 = keep.tile([P, 8], F32)
+        gain = keep.tile([P, 8], F32)
+        c0_col = keep.tile([P, R], F32)
+
+        def constants():
+            nc.vector.reciprocal(inv_cap[:], flat(vec["cap"]))
+            nc.vector.tensor_scalar(out=gain[:], in0=flat(vec["t0"]), scalar1=0.15, scalar2=None, op0=ALU.mult)
+            nc.vector.tensor_tensor(out=base[:], in0=flat(vec["f0"]), in1=inv_cap[:], op=ALU.mult)
+            nc.vector.tensor_copy(out=c0_col[:], in_=c0_bf[:])
+            nc.vector.tensor_tensor(out=base2[:], in0=base[:], in1=base[:], op=ALU.mult)
+            nc.vector.tensor_tensor(out=base4[:], in0=base2[:], in1=base2[:], op=ALU.mult)
+
+        xg, xc, xs, ec, es, cc, negm, y, yw, ysc, q, e16, eg, low, bank, w, inv, inv_t, total, total_s, u, yb, acc, prod, prod2, rec, done_y = ({} for _ in range(27))
+
+        def turn_x(g, t):
+            if g not in xg:
+                xg[g] = keep.tile([P, 2, HALF, 4], BF16, name="xg", align_bytes=64)
+            words = x_sb[g][:].rearrange("p t k -> p (t k)").bitcast(F32)
+            bank[g, t] = turn.tile([P, 4, P], F32, name="bank")
+            for k in range(2):
+                for uu in range(2):
+                    lo = HALF * t + 256 * k
+                    nc.tensor.transpose(bank[g, t][:, 2 * k + uu, :], words[:, lo + uu : lo + 256 : 2], ident[:])
+
+        def copy_x(g, t, eng):
+            out = xg[g][:].rearrange("p k n j -> p (k n j)").bitcast(F32)
+            out = out.rearrange("p (k n u) -> p k n u", k=2, u=2)[:, :, P * t : P * (t + 1), :]
+            src = bank[g, t][:].rearrange("p (k u) m -> p k m u", k=2)
+            if eng == "act":
+                nc.scalar.copy(out=out, in_=src)
+            else:
+                nc.vector.tensor_copy(out=out, in_=src)
+
+        def quant_x(g, k):
+            if g not in xc:
+                xc[g] = two.tile([P, 2, HALF], U32, name="xc", align_bytes=64)
+                xs[g] = two.tile([P, 2, HALF], U8, name="xs", align_bytes=64)
+            nc.vector.quantize_mx(
+                out=xc[g][:, k, :].bitcast(FP8X4),
+                scales=xs[g][:, k, :],
+                in_=xg[g][:, k, :, :].rearrange("p n j -> p (n j)"),
+            )
+
+        def mm1(g, h, t):
+            if (g, h) not in q:
+                q[g, h] = two.tile([P, 4, HALF], F32, name="q")
+            a = acc[g, h, t] = mm.tile([P, HALF], F32, name="acc")
+            col = HALF * h + P * t
+            for k in range(2):
+                nc.tensor.matmul_mx(
+                    out=a[:],
+                    lhsT=dw[:, k, 2 * col : 2 * (col + P)].bitcast(FP4X4),
+                    lhsT_scale=ds[:, k, col : col + P],
+                    rhs=xc[g][:, k, :].bitcast(FP8X4),
+                    rhs_scale=xs[g][:, k, :],
+                    start=(k == 0),
+                    stop=(k == 1),
+                )
+
+        def sq1(g, h, t):
+            j = 4 * h + t
+            nc.scalar.activation(
+                out=q[g, h][:, t, :], in_=acc[g, h, t][:], func=ACT.Square,
+                scale=inv_cap[:, j : j + 1], bias=base[:, j : j + 1],
+            )
+
+        def sq2(g, h, i, eng="act"):
+            v = q[g, h][:, 2 * i : 2 * i + 2, :]
+            if eng == "act":
+                nc.scalar.activation(out=v, in_=v, func=ACT.Square)
+            else:
+                nc.vector.tensor_tensor(out=v, in0=v, in1=v, op=ALU.mult)
+
+        def affine(g, h, t):
+            j = 4 * h + t
+            if (g, h) not in e16:
+                e16[g, h] = two.tile([P, 4, HALF], BF16, name="e16", align_bytes=64)
+            nc.vector.tensor_scalar(
+                out=e16[g, h][:, t, :], in0=q[g, h][:, t, :],
+                scalar1=base4[:, j : j + 1], scalar2=gain[:, j : j + 1],
+                op0=ALU.subtract, op1=ALU.mult,
+            )
+
+        def weave_e(g, h):
+            eg[g, h] = two.tile([P, HALF, 4], BF16, name="eg", align_bytes=64)
+            nc.vector.tensor_copy(
+                out=eg[g, h][:].rearrange("p (c i) t -> p c t i", i=4),
+                in_=e16[g, h][:].rearrange("p t (c i) -> p c t i", i=4),
+            )
+
+        def quant_e(g, h):
+            if g not in ec:
+                ec[g] = two.tile([P, 2, HALF], U32, name="ec", align_bytes=64)
+                es[g] = two.tile([P, 2, HALF], U8, name="es", align_bytes=64)
+            nc.vector.quantize_mx(
+                out=ec[g][:, h, :].bitcast(FP8X4), scales=es[g][:, h, :],
+                in_=eg[g, h][:].rearrange("p n j -> p (n j)"),
+            )
+
+        def mm2(g, r):
+            a = acc[g, r] = mm.tile([P, HALF], F32, name="acc")
+            for k in range(2):
+                nc.tensor.matmul_mx(
+                    out=a[:],
+                    lhsT=pw[:, k, 256 * r : 256 * (r + 1)].bitcast(FP4X4),
+                    lhsT_scale=psc[:, k, P * r : P * (r + 1)],
+                    rhs=ec[g][:, k, :].bitcast(FP8X4),
+                    rhs_scale=es[g][:, k, :],
+                    start=(k == 0),
+                    stop=(k == 1),
+                )
+
+        def leave(g, r):
+            if g not in cc:
+                cc[g] = two.tile([P, R, HALF], F32, name="cc")
+            nc.scalar.activation(
+                out=cc[g][:, r, :], in_=acc[g, r][:], func=ACT.Identity, scale=1.0, bias=c0_col[:, r : r + 1]
+            )
+
+        def low1(g, i):
+            if g not in low:
+                low[g] = keep.tile([P, 4, HALF], F32, name="low")
+                negm[g] = two.tile([P, HALF], F32, name="negm")
+            nc.vector.tensor_tensor(out=low[g][:, i, :], in0=cc[g][:, i, :], in1=cc[g][:, i + 4, :], op=ALU.min)
+
+        def low2(g, i):
+            nc.vector.tensor_tensor(
+                out=low[g][:, i, :] if i < 3 else negm[g][:], in0=low[g][:, i - 1, :], in1=low[g][:, i, :], op=ALU.min
+            )
+
+        def low3(g):
+            pass
+
+        def low4(g):
+            nc.vector.tensor_scalar(out=negm[g][:], in0=negm[g][:], scalar1=-1.0, scalar2=None, op0=ALU.mult)
+
+        def turn_d(g, t, hf):
+            cols = slice(P * t, P * (t + 1))
+            b = bank[g, t, hf] = turn.tile([P, 4, P], F32, name="bank")
+            for i in range(4):
+                nc.tensor.matmul(b[:, i, :], cc[g][:, 4 * hf + i, cols], ident[:], start=True, stop=False, is_transpose=True)
+                nc.tensor.matmul(b[:, i, :], negm[g][:, cols], ident[:], start=False, stop=True, is_transpose=True)
+
+        def expo(g, t, hf):
+            if (g, t) not in w:
+                w[g, t] = five.tile([P, R, P], F32, name="w")
+            nc.scalar.activation(
+                out=w[g, t][:, 4 * hf : 4 * hf + 4, :], in_=bank[g, t, hf][:], func=ACT.Exp, scale=-1.0
+            )
+
+        def sums(g, t, t0_, n):
+            if (g, t0_) not in total:
+                total[g, t0_] = small.tile([P, 4, P], F32, name="total")
+            s = total[g, t0_][:, t - t0_, :]
+            for r in range(R):
+                nc.tensor.matmul(s, w[g, t][:, r, :], ident[:], start=(r == 0), stop=(r == R - 1), is_transpose=True)
+
+        def sums_out(g, t0_, n):
+            total_s[g, t0_] = two.tile([P, n, P], F32, name="total_s%d" % n)
+            nc.scalar.copy(out=total_s[g, t0_][:], in_=total[g, t0_][:, 0:n, :])
+
+        def mul(out, in0, in1):
+            nc.vector.tensor_tensor(out=out, in0=in0, in1=in1, op=ALU.mult)
+
+        def invert_a(g, t0_, n):
+            s = total_s[g, t0_]
+            prod[g, t0_] = two.tile([P, 3, P], F32, name="prod")
+            if n == 4:
+                mul(prod[g, t0_][:, 0:2, :], s[:, 0:2, :], s[:, 2:4, :])
+            else:
+                mul(prod[g, t0_][:, 2, :], s[:, 0, :], s[:, 1, :])
+
+        def invert_b(g, t0_):
+            mul(prod[g, t0_][:, 2, :], prod[g, t0_][:, 0, :], prod[g, t0_][:, 1, :])
+
+        def invert_c(g, t0_):
+            rec[g, t0_] = two.tile([P, P], F32, name="rec")
+            nc.vector.reciprocal(rec[g, t0_][:], prod[g, t0_][:, 2, :])
+
+        def invert_d(g, t0_):
+            pr = prod2[g, t0_] = two.tile([P, 2, P], F32, name="prod2")
+            mul(pr[:, 0, :], rec[g, t0_][:], prod[g, t0_][:, 1, :])
+            mul(pr[:, 1, :], rec[g, t0_][:], prod[g, t0_][:, 0, :])
+
+        def invert_e(g, t0_, n):
+            s = total_s[g, t0_]
+            iv = inv[g, t0_] = two.tile([P, n, P], F32, name="inv%d" % n)
+            if n == 4:
+                mul(iv[:, 0:2, :], prod2[g, t0_][:], s[:, 2:4, :])
+                mul(iv[:, 2:4, :], prod2[g, t0_][:], s[:, 0:2, :])
+            else:
+                mul(iv[:, 0, :], rec[g, t0_][:], s[:, 1, :])
+                mul(iv[:, 1, :], rec[g, t0_][:], s[:, 0, :])
+
+        def turn_inv(g, t0_, n):
+            it = total[g, t0_][:, 2:4, :]
+            for i in range(n):
+                nc.tensor.transpose(it[:, i, :], inv[g, t0_][:, i, :], ident[:])
+                inv_t[g, t0_ + i] = it[:, i, :]
+
+        def share(g, t, hf):
+            if (g, t) not in u:
+                u[g, t] = two.tile([P, P, R], F32, name="u")
+            nc.vector.tensor_tensor(
+                out=u[g, t][:, :, 4 * hf : 4 * hf + 4],
+                in0=w[g, t][:, 4 * hf : 4 * hf + 4, :].rearrange("m r o -> m o r"),
+                in1=inv_t[g, t].unsqueeze(2).to_broadcast([P, P, 4]),
+                op=ALU.mult,
+            )
+
+        def result(g, t, eng):
+            if g not in y:
+                y[g] = two.tile([P, 4, D], F32, name="y")
+            src = u[g, t][:].rearrange("m o r -> m (o r)")
+            if eng == "act":
+                nc.scalar.activation(out=y[g][:, t, :], in_=src, func=ACT.Copy, scale=8.0, bias=-1.0)
+            elif eng == "pool":
+                nc.gpsimd.tensor_scalar(
+                    out=y[g][:, t, :], in0=src, scalar1=8.0, scalar2=-1.0, op0=ALU.mult, op1=ALU.add
+                )
+            else:
+                nc.vector.tensor_scalar(
+                    out=y[g][:, t, :], in0=src, scalar1=8.0, scalar2=-1.0, op0=ALU.mult, op1=ALU.add
+                )
+            nc.sync.dma_start(
+                out=out_0.rearrange("(g m t) p -> g m t p", g=2, t=4)[g, :, t, :], in_=y[g][:, t, :]
+            )
+
+        def weave_y(g, c, eng):
+            if g not in yw:
+                yw[g] = two.tile([P, D], U32, name="yw", align_bytes=64)
+                ysc[g] = two.tile([P, D], U8, name="ysc", align_bytes=64)
+                nc.gpsimd.memset(ysc[g][:].bitcast(I32), 0)
+            yb[g, c] = three.tile([P, 256, 4], BF16, name="yb", align_bytes=64)
+            cols = slice(256 * c, 256 * (c + 1))
+            out = yb[g, c][:].rearrange("p (c i) t -> p c t i", i=4)
+            src = y[g][:, :, cols].rearrange("p t (c i) -> p c t i", i=4)
+            if eng == "act":
+                nc.scalar.copy(out=out, in_=src)
+            elif eng == "pool":
+                nc.gpsimd.tensor_scalar(out=out, in0=src, scalar1=1.0, scalar2=0.0, op0=ALU.mult, op1=ALU.add)
+            else:
+                nc.vector.tensor_copy(out=out, in_=src)
+
+        def quant_y(g, c):
+            cols = slice(256 * c, 256 * (c + 1))
+            nc.vector.quantize_mx(
+                out=yw[g][:, cols].bitcast(FP8X4), scales=ysc[g][:, cols],
+                in_=yb[g, c][:].rearrange("p n j -> p (n j)"),
+            )
+            nc.sync.dma_start(
+                out=out_1[g].rearrange("m p t -> m (p t)").bitcast(I32)[:, cols], in_=yw[g][:, cols].bitcast(I32)
+            )
+            done_y[g] = done_y.get(g, 0) + 1
+            if done_y[g] == 4:
+                for qd in range(4):
+                    nc.sync.dma_start(
+                        out=out_2[g, 4 * qd : 4 * qd + 4, :].bitcast(I32),
+                        in_=ysc[g][32 * qd : 32 * qd + 4, :].bitcast(I32),
+                    )
+
+
+        def m1(g, h, *ts):
+            for t in ts:
+                mm1(g, h, t)
+                sq1(g, h, t)
+
+        def aff(g, h, *ts):
+            for t in ts:
+                affine(g, h, t)
+
+        def turn_pair(g, t):
+            turn_d(g, t, 0)
+            turn_d(g, t, 1)
+
+        def expos(g, t):
+            expo(g, t, 0)
+            expo(g, t, 1)
+
+        def inverse(g, t0_):
+            invert_a(g, t0_, 2)
+            invert_c(g, t0_)
+            invert_e(g, t0_, 2)
+            turn_inv(g, t0_, 2)
+
+        def leave_pair(g, i):
+            mm2(g, i)
+            mm2(g, i + 4)
+            leave(g, i)
+            leave(g, i + 4)
+
+        def shares(g, t):
+            share(g, t, 0)
+            share(g, t, 1)
+
+        with tc.manual_schedule():
+            perm_dlt(0)
+            constants()
+            perm_dlt(1)
+            for t in range(4):
+                turn_x(0, t)
+                copy_x(0, t, "act")
+            quant_x(0, 0)
+            quant_x(0, 1)
+            mm1(0, 0, 0)
+            mm1(0, 0, 1)
+            mm1(0, 0, 2)
+            turn_x(1, 0)
+            turn_x(1, 1)
+            sq1(0, 0, 0)
+            sq1(0, 0, 1)
+            mm1(0, 0, 3)
+            perm_perc_words(0)
+            sq1(0, 0, 2)
+            sq2(0, 0, 0)
+            sq1(0, 0, 3)
+            copy_x(1, 0, "dve")
+            copy_x(1, 1, "act")
+            mm1(0, 1, 0)
+            turn_x(1, 2)
+            turn_x(1, 3)
+            sq2(0, 0, 1)
+            aff(0, 0, 0, 1)
+            copy_x(1, 2, "dve")
+            mm1(0, 1, 1)
+            mm1(0, 1, 2)
+            sq1(0, 1, 0)
+            copy_x(1, 3, "act")
+            aff(0, 0, 2, 3)
+            sq1(0, 1, 1)
+            mm1(0, 1, 3)
+            sq1(0, 1, 2)
+            weave_e(0, 0)
+            sq2(0, 1, 0)
+            sq1(0, 1, 3)
+            quant_x(1, 0)
+            sq2(0, 1, 1)
+            quant_x(1, 1)
+            quant_e(0, 0)
+            perm_perc_words(1)
+            aff(0, 1, 0, 1)
+            perm_perc_scales(0)
+            mm1(1, 0, 0)
+            mm1(1, 0, 1)
+            mm1(1, 0, 2)
+            sq1(1, 0, 0)
+            sq1(1, 0, 1)
+            aff(0, 1, 2, 3)
+            perm_perc_scales(1)
+            weave_e(0, 1)
+            sq2(1, 0, 0)
+            sq1(1, 0, 2)
+            mm1(1, 0, 3)
+            quant_e(0, 1)
+            sq1(1, 0, 3)
+            leave_pair(0, 0)
+            sq2(1, 0, 1, "dve")
+            aff(1, 0, 0, 1)
+            leave_pair(0, 1)
+            low1(0, 0)
+            aff(1, 0, 2, 3)
+            leave_pair(0, 2)
+            low1(0, 1)
+            low2(0, 1)
+            weave_e(1, 0)
+            leave_pair(0, 3)
+            low1(0, 2)
+            low2(0, 2)
+            low1(0, 3)
+            m1(1, 1, 0, 1)
+            sq2(1, 1, 0)
+            quant_e(1, 0)
+            low2(0, 3)
+            low4(0)
+            m1(1, 1, 2, 3)
+            sq2(1, 1, 1, "dve")
+            turn_pair(0, 0)
+            expos(0, 0)
+            aff(1, 1, 0, 1)
+            turn_pair(0, 1)
+            sums(0, 0, 0, 2)
+            expos(0, 1)
+            aff(1, 1, 2, 3)
+            weave_e(1, 1)
+            sums(0, 1, 0, 2)
+            sums_out(0, 0, 2)
+            quant_e(1, 1)
+            invert_a(0, 0, 2)
+            invert_c(0, 0)
+            mm2(1, 0)
+            mm2(1, 4)
+            leave(1, 0)
+            leave(1, 4)
+            mm2(1, 1)
+            invert_e(0, 0, 2)
+            turn_inv(0, 0, 2)
+            mm2(1, 5)
+            leave(1, 1)
+            leave(1, 5)
+            low1(1, 0)
+            turn_pair(0, 2)
+            shares(0, 0)
+            result(0, 0, "pool")
+            leave_pair(1, 2)
+            low1(1, 1)
+            low2(1, 1)
+            leave_pair(1, 3)
+            expos(0, 2)
+            turn_pair(0, 3)
+            sums(0, 2, 2, 2)
+            expos(0, 3)
+            sums(0, 3, 2, 2)
+            sums_out(0, 2, 2)
+            shares(0, 1)
+            result(0, 1, "pool")
+            low1(1, 2)
+            low2(1, 2)
+            low1(1, 3)
+            low2(1, 3)
+            low4(1)
+            turn_pair(1, 0)
+            expos(1, 0)
+            turn_pair(1, 1)
+            invert_a(0, 2, 2)
+            invert_c(0, 2)
+            invert_e(0, 2, 2)
+            sums(1, 0, 0, 2)
+            turn_inv(0, 2, 2)
+            expos(1, 1)
+            shares(0, 2)
+            result(0, 2, "act")
+            turn_pair(1, 2)
+            sums(1, 1, 0, 2)
+            sums_out(1, 0, 2)
+            expos(1, 2)
+            turn_pair(1, 3)
+            shares(0, 3)
+            result(0, 3, "pool")
+            invert_a(1, 0, 2)
+            invert_c(1, 0)
+            invert_e(1, 0, 2)
+            turn_inv(1, 0, 2)
+            sums(1, 2, 2, 2)
+            expos(1, 3)
+            sums(1, 3, 2, 2)
+            sums_out(1, 2, 2)
+            weave_y(0, 0, "act")
+            shares(1, 0)
+            result(1, 0, "pool")
+            weave_y(0, 1, "act")
+            invert_a(1, 2, 2)
+            invert_c(1, 2)
+            invert_e(1, 2, 2)
+            turn_inv(1, 2, 2)
+            shares(1, 1)
+            result(1, 1, "act")
+            quant_y(0, 0)
+            quant_y(0, 1)
+            weave_y(0, 2, "act")
+            shares(1, 2)
+            result(1, 2, "act")
+            weave_y(0, 3, "dve")
+            shares(1, 3)
+            result(1, 3, "act")
+            quant_y(0, 2)
+            quant_y(0, 3)
+            weave_y(1, 0, "dve")
+            weave_y(1, 1, "act")
+            weave_y(1, 2, "dve")
+            quant_y(1, 0)
+            weave_y(1, 3, "act")
+            quant_y(1, 2)
+            quant_y(1, 1)
+            quant_y(1, 3)

@@ -30,10 +30,10 @@ def tile_bprexcessdelaylogitroutesplit_x2_kernel(
         keep = ctx.enter_context(tc.tile_pool(name="keep", bufs=1))
         two = ctx.enter_context(tc.tile_pool(name="two", bufs=2))
         five = ctx.enter_context(tc.tile_pool(name="five", bufs=5))
+        four = ctx.enter_context(tc.tile_pool(name="four", bufs=4))
         three = ctx.enter_context(tc.tile_pool(name="three", bufs=3))
-        turn = ctx.enter_context(tc.psum_pool(name="turn", bufs=3))
-        mm = ctx.enter_context(tc.psum_pool(name="mm", bufs=3))
-        small = ctx.enter_context(tc.psum_pool(name="small", bufs=2))
+        turn = ctx.enter_context(tc.psum_pool(name="turn", bufs=4))
+        mm = ctx.enter_context(tc.psum_pool(name="mm", bufs=4))
 
         x_rows = x.rearrange("(g m t) k -> g m t k", g=2, t=4)
         x_sb = [keep.tile([P, 4, D], BF16, name="x_sb%d" % g, align_bytes=64) for g in range(2)]
@@ -56,26 +56,29 @@ def tile_bprexcessdelaylogitroutesplit_x2_kernel(
                     in_=src[:, 4 * q : 4 * q + 4, :].bitcast(I32).rearrange("g q w -> q g w"),
                 )
 
-        nc.vector.memset(raw_s["dlt"][:].rearrange("p g n -> p (g n)").bitcast(I32), 0)
-        nc.vector.memset(raw_s["perc"][:].rearrange("p g n -> p (g n)").bitcast(I32), 0)
-        load_scales("dlt", dlt_scales, nc.scalar)
-        load_words("dlt", dlt_words, 0)
-        load_words("dlt", dlt_words, 1)
-        load_scales("perc", perc_scales, nc.gpsimd)
-        for t in range(4):
-            nc.sync.dma_start(out=x_sb[0][:, t, :], in_=x_rows[0, :, t, :])
-        load_words("perc", perc_words, 0)
-        load_words("perc", perc_words, 1)
-        for key, src in (("f0", f0), ("cap", cap), ("t0", t0)):
-            vec[key] = keep.tile([P, 2, 4], BF16, name="v_" + key)
-            nc.gpsimd.dma_start(out=vec[key][:], in_=src.rearrange("(h p t) -> p h t", h=2, t=4))
-        c0_bf = keep.tile([P, R], BF16)
-        nc.gpsimd.dma_start(out=c0_bf[:], in_=c0.rearrange("(o r) -> o r", r=R))
-        for t in range(4):
-            nc.sync.dma_start(out=x_sb[1][:, t, :], in_=x_rows[1, :, t, :])
-
         ident = keep.tile([P, P], F32)
         make_identity(nc, ident[:])
+        blank = keep.tile([P, HALF], BF16, align_bytes=64)
+        nc.vector.memset(blank[:], 0.0)
+        nc.vector.memset(raw_s["dlt"][:].rearrange("p g n -> p (g n)").bitcast(I32), 0)
+        nc.vector.memset(raw_s["perc"][:].rearrange("p g n -> p (g n)").bitcast(I32), 0)
+        load_words("dlt", dlt_words, 0)
+        load_words("dlt", dlt_words, 1)
+        for key, src in (("cap", cap), ("f0", f0)):
+            vec[key] = keep.tile([P, 2, 4], BF16, name="v_" + key)
+            nc.scalar.dma_start(out=vec[key][:], in_=src.rearrange("(h p t) -> p h t", h=2, t=4))
+        load_scales("dlt", dlt_scales, nc.scalar)
+        for t in range(4):
+            nc.sync.dma_start(out=x_sb[0][:, t, :], in_=x_rows[0, :, t, :])
+        vec["t0"] = keep.tile([P, 2, 4], BF16, name="v_t0")
+        nc.gpsimd.dma_start(out=vec["t0"][:], in_=t0.rearrange("(h p t) -> p h t", h=2, t=4))
+        c0_bf = keep.tile([P, R], BF16)
+        nc.gpsimd.dma_start(out=c0_bf[:], in_=c0.rearrange("(o r) -> o r", r=R))
+        load_scales("perc", perc_scales, nc.gpsimd)
+        load_words("perc", perc_words, 0)
+        load_words("perc", perc_words, 1)
+        for t in range(4):
+            nc.sync.dma_start(out=x_sb[1][:, t, :], in_=x_rows[1, :, t, :])
 
         dw = keep.tile([P, 2, 2 * D], U8, align_bytes=64)
         ds = keep.tile([P, 2, D], U8, align_bytes=64)
@@ -114,6 +117,7 @@ def tile_bprexcessdelaylogitroutesplit_x2_kernel(
         base2 = keep.tile([P, 8], F32)
         base4 = keep.tile([P, 8], F32)
         gain = keep.tile([P, 8], F32)
+        shift = keep.tile([P, 8], F32)
         c0_col = keep.tile([P, R], F32)
 
         def constants():
@@ -123,8 +127,27 @@ def tile_bprexcessdelaylogitroutesplit_x2_kernel(
             nc.vector.tensor_copy(out=c0_col[:], in_=c0_bf[:])
             nc.vector.tensor_tensor(out=base2[:], in0=base[:], in1=base[:], op=ALU.mult)
             nc.vector.tensor_tensor(out=base4[:], in0=base2[:], in1=base2[:], op=ALU.mult)
+            nc.vector.scalar_tensor_tensor(out=shift[:], in0=base4[:], scalar=-1.0, in1=gain[:], op0=ALU.mult, op1=ALU.mult)
 
-        xg, xc, xs, ec, es, cc, negm, y, yw, ysc, q, e16, eg, low, bank, w, inv, inv_t, total, total_s, u, yb, acc, prod, prod2, rec, done_y = ({} for _ in range(27))
+        xg, xc, xs, ec, es, cc, negm, y, yw, ysc, q, e16, eg, low, bank, w, inv, inv_t, total, total_s, u, yb, acc, prod, prod2, rec, done_y, part = ({} for _ in range(28))
+
+        def warm(n, k, eng):
+            for _ in range(n if eng == "on" else 0):
+                idle = mm.tile([P, HALF], F32, name="acc")
+                nc.tensor.matmul(idle[:], blank[:, 0:P], blank[:], start=True, stop=True)
+
+        def heat(n, k, eng):
+            for _ in range(n if eng == "on" else 0):
+                idle = mm.tile([P, HALF], F32, name="acc")
+                nc.tensor.matmul_mx(
+                    out=idle[:],
+                    lhsT=dw[:, 0, 0:256].bitcast(FP4X4),
+                    lhsT_scale=ds[:, 0, 0:P],
+                    rhs=xc[0][:, 0, :].bitcast(FP8X4),
+                    rhs_scale=xs[0][:, 0, :],
+                    start=True,
+                    stop=True,
+                )
 
         def turn_x(g, t):
             if g not in xg:
@@ -178,29 +201,37 @@ def tile_bprexcessdelaylogitroutesplit_x2_kernel(
                 scale=inv_cap[:, j : j + 1], bias=base[:, j : j + 1],
             )
 
-        def sq2(g, h, i, eng="act"):
+        def sq2(g, h, i, eng):
             v = q[g, h][:, 2 * i : 2 * i + 2, :]
             if eng == "act":
                 nc.scalar.activation(out=v, in_=v, func=ACT.Square)
             else:
                 nc.vector.tensor_tensor(out=v, in0=v, in1=v, op=ALU.mult)
 
-        def affine(g, h, t):
+        def affine(g, h, t, eng):
             j = 4 * h + t
             if (g, h) not in e16:
                 e16[g, h] = two.tile([P, 4, HALF], BF16, name="e16", align_bytes=64)
-            nc.vector.tensor_scalar(
-                out=e16[g, h][:, t, :], in0=q[g, h][:, t, :],
-                scalar1=base4[:, j : j + 1], scalar2=gain[:, j : j + 1],
-                op0=ALU.subtract, op1=ALU.mult,
-            )
+            if eng == "act":
+                nc.scalar.activation(
+                    out=e16[g, h][:, t, :], in_=q[g, h][:, t, :], func=ACT.Identity,
+                    scale=gain[:, j : j + 1], bias=shift[:, j : j + 1],
+                )
+            else:
+                nc.vector.tensor_scalar(
+                    out=e16[g, h][:, t, :], in0=q[g, h][:, t, :],
+                    scalar1=base4[:, j : j + 1], scalar2=gain[:, j : j + 1],
+                    op0=ALU.subtract, op1=ALU.mult,
+                )
 
-        def weave_e(g, h):
+        def weave_e(g, h, eng):
             eg[g, h] = two.tile([P, HALF, 4], BF16, name="eg", align_bytes=64)
-            nc.vector.tensor_copy(
-                out=eg[g, h][:].rearrange("p (c i) t -> p c t i", i=4),
-                in_=e16[g, h][:].rearrange("p t (c i) -> p c t i", i=4),
-            )
+            out = eg[g, h][:].rearrange("p (c i) t -> p c t i", i=4)
+            src = e16[g, h][:].rearrange("p t (c i) -> p c t i", i=4)
+            if eng == "act":
+                nc.scalar.copy(out=out, in_=src)
+            else:
+                nc.vector.tensor_copy(out=out, in_=src)
 
         def quant_e(g, h):
             if g not in ec:
@@ -224,12 +255,17 @@ def tile_bprexcessdelaylogitroutesplit_x2_kernel(
                     stop=(k == 1),
                 )
 
-        def leave(g, r):
+        def leave(g, r, eng):
             if g not in cc:
                 cc[g] = two.tile([P, R, HALF], F32, name="cc")
-            nc.scalar.activation(
-                out=cc[g][:, r, :], in_=acc[g, r][:], func=ACT.Identity, scale=1.0, bias=c0_col[:, r : r + 1]
-            )
+            if eng == "act":
+                nc.scalar.activation(
+                    out=cc[g][:, r, :], in_=acc[g, r][:], func=ACT.Identity, scale=1.0, bias=c0_col[:, r : r + 1]
+                )
+            else:
+                nc.vector.tensor_scalar(
+                    out=cc[g][:, r, :], in0=acc[g, r][:], scalar1=c0_col[:, r : r + 1], scalar2=None, op0=ALU.add
+                )
 
         def low1(g, i):
             if g not in low:
@@ -242,11 +278,11 @@ def tile_bprexcessdelaylogitroutesplit_x2_kernel(
                 out=low[g][:, i, :] if i < 3 else negm[g][:], in0=low[g][:, i - 1, :], in1=low[g][:, i, :], op=ALU.min
             )
 
-        def low3(g):
-            pass
-
-        def low4(g):
-            nc.vector.tensor_scalar(out=negm[g][:], in0=negm[g][:], scalar1=-1.0, scalar2=None, op0=ALU.mult)
+        def low4(g, eng):
+            if eng == "act":
+                nc.scalar.activation(out=negm[g][:], in_=negm[g][:], func=ACT.Copy, scale=-1.0)
+            else:
+                nc.vector.tensor_scalar(out=negm[g][:], in0=negm[g][:], scalar1=-1.0, scalar2=None, op0=ALU.mult)
 
         def turn_d(g, t, hf):
             cols = slice(P * t, P * (t + 1))
@@ -262,16 +298,21 @@ def tile_bprexcessdelaylogitroutesplit_x2_kernel(
                 out=w[g, t][:, 4 * hf : 4 * hf + 4, :], in_=bank[g, t, hf][:], func=ACT.Exp, scale=-1.0
             )
 
-        def sums(g, t, t0_, n):
-            if (g, t0_) not in total:
-                total[g, t0_] = small.tile([P, 4, P], F32, name="total")
-            s = total[g, t0_][:, t - t0_, :]
-            for r in range(R):
-                nc.tensor.matmul(s, w[g, t][:, r, :], ident[:], start=(r == 0), stop=(r == R - 1), is_transpose=True)
+        def fold1(g, t):
+            part[g, t] = two.tile([P, 6, P], F32, name="part")
+            nc.vector.tensor_tensor(
+                out=part[g, t][:, 0:4, :], in0=w[g, t][:, 0:4, :], in1=w[g, t][:, 4:8, :], op=ALU.add
+            )
 
-        def sums_out(g, t0_, n):
-            total_s[g, t0_] = two.tile([P, n, P], F32, name="total_s%d" % n)
-            nc.scalar.copy(out=total_s[g, t0_][:], in_=total[g, t0_][:, 0:n, :])
+        def fold2(g, t):
+            pt = part[g, t]
+            nc.vector.tensor_tensor(out=pt[:, 4:6, :], in0=pt[:, 0:2, :], in1=pt[:, 2:4, :], op=ALU.add)
+
+        def fold3(g, t, t0_):
+            if (g, t0_) not in total_s:
+                total_s[g, t0_] = two.tile([P, 2, P], F32, name="total_s")
+            pt = part[g, t]
+            nc.vector.tensor_tensor(out=total_s[g, t0_][:, t - t0_, :], in0=pt[:, 4, :], in1=pt[:, 5, :], op=ALU.add)
 
         def mul(out, in0, in1):
             nc.vector.tensor_tensor(out=out, in0=in0, in1=in1, op=ALU.mult)
@@ -306,19 +347,13 @@ def tile_bprexcessdelaylogitroutesplit_x2_kernel(
                 mul(iv[:, 0, :], rec[g, t0_][:], s[:, 1, :])
                 mul(iv[:, 1, :], rec[g, t0_][:], s[:, 0, :])
 
-        def turn_inv(g, t0_, n):
-            it = total[g, t0_][:, 2:4, :]
-            for i in range(n):
-                nc.tensor.transpose(it[:, i, :], inv[g, t0_][:, i, :], ident[:])
-                inv_t[g, t0_ + i] = it[:, i, :]
-
         def share(g, t, hf):
             if (g, t) not in u:
                 u[g, t] = two.tile([P, P, R], F32, name="u")
             nc.vector.tensor_tensor(
                 out=u[g, t][:, :, 4 * hf : 4 * hf + 4],
                 in0=w[g, t][:, 4 * hf : 4 * hf + 4, :].rearrange("m r o -> m o r"),
-                in1=inv_t[g, t].unsqueeze(2).to_broadcast([P, P, 4]),
+                in1=inv[g, 2 * (t // 2)][:, t % 2, :].unsqueeze(2).to_broadcast([P, P, 4]),
                 op=ALU.mult,
             )
 
@@ -345,7 +380,7 @@ def tile_bprexcessdelaylogitroutesplit_x2_kernel(
                 yw[g] = two.tile([P, D], U32, name="yw", align_bytes=64)
                 ysc[g] = two.tile([P, D], U8, name="ysc", align_bytes=64)
                 nc.gpsimd.memset(ysc[g][:].bitcast(I32), 0)
-            yb[g, c] = three.tile([P, 256, 4], BF16, name="yb", align_bytes=64)
+            yb[g, c] = four.tile([P, 256, 4], BF16, name="yb", align_bytes=64)
             cols = slice(256 * c, 256 * (c + 1))
             out = yb[g, c][:].rearrange("p (c i) t -> p c t i", i=4)
             src = y[g][:, :, cols].rearrange("p t (c i) -> p c t i", i=4)
@@ -374,215 +409,259 @@ def tile_bprexcessdelaylogitroutesplit_x2_kernel(
                     )
 
 
-        def m1(g, h, *ts):
-            for t in ts:
-                mm1(g, h, t)
-                sq1(g, h, t)
-
-        def aff(g, h, *ts):
-            for t in ts:
-                affine(g, h, t)
-
-        def turn_pair(g, t):
-            turn_d(g, t, 0)
-            turn_d(g, t, 1)
-
-        def expos(g, t):
-            expo(g, t, 0)
-            expo(g, t, 1)
-
-        def inverse(g, t0_):
-            invert_a(g, t0_, 2)
-            invert_c(g, t0_)
-            invert_e(g, t0_, 2)
-            turn_inv(g, t0_, 2)
-
-        def leave_pair(g, i):
-            mm2(g, i)
-            mm2(g, i + 4)
-            leave(g, i)
-            leave(g, i + 4)
-
-        def shares(g, t):
-            share(g, t, 0)
-            share(g, t, 1)
-
         with tc.manual_schedule():
             perm_dlt(0)
-            constants()
+            warm(6, 0, "on")
+            warm(0, 1, "on")
+            turn_x(0, 0)
+            copy_x(0, 0, "act")
             perm_dlt(1)
-            for t in range(4):
-                turn_x(0, t)
-                copy_x(0, t, "act")
-            quant_x(0, 0)
+            turn_x(0, 1)
+            copy_x(0, 1, "act")
+            turn_x(0, 2)
+            copy_x(0, 2, "act")
+            turn_x(0, 3)
+            copy_x(0, 3, "dve")
             quant_x(0, 1)
-            mm1(0, 0, 0)
-            mm1(0, 0, 1)
-            mm1(0, 0, 2)
-            turn_x(1, 0)
             turn_x(1, 1)
-            sq1(0, 0, 0)
-            sq1(0, 0, 1)
-            mm1(0, 0, 3)
-            perm_perc_words(0)
-            sq1(0, 0, 2)
-            sq2(0, 0, 0)
-            sq1(0, 0, 3)
-            copy_x(1, 0, "dve")
-            copy_x(1, 1, "act")
-            mm1(0, 1, 0)
-            turn_x(1, 2)
-            turn_x(1, 3)
-            sq2(0, 0, 1)
-            aff(0, 0, 0, 1)
-            copy_x(1, 2, "dve")
-            mm1(0, 1, 1)
-            mm1(0, 1, 2)
-            sq1(0, 1, 0)
-            copy_x(1, 3, "act")
-            aff(0, 0, 2, 3)
-            sq1(0, 1, 1)
-            mm1(0, 1, 3)
-            sq1(0, 1, 2)
-            weave_e(0, 0)
-            sq2(0, 1, 0)
-            sq1(0, 1, 3)
-            quant_x(1, 0)
-            sq2(0, 1, 1)
-            quant_x(1, 1)
-            quant_e(0, 0)
+            quant_x(0, 0)
+            constants()
             perm_perc_words(1)
-            aff(0, 1, 0, 1)
+            copy_x(1, 1, "act")
+            mm1(0, 0, 2)
+            perm_perc_words(0)
+            mm1(0, 0, 1)
+            sq1(0, 0, 2)
+            sq1(0, 0, 1)
+            mm1(0, 0, 0)
+            mm1(0, 0, 3)
             perm_perc_scales(0)
-            mm1(1, 0, 0)
-            mm1(1, 0, 1)
-            mm1(1, 0, 2)
-            sq1(1, 0, 0)
-            sq1(1, 0, 1)
-            aff(0, 1, 2, 3)
+            sq1(0, 0, 0)
+            sq2(0, 0, 0, "dve")
+            sq1(0, 0, 3)
+            sq2(0, 0, 1, "dve")
+            mm1(0, 1, 1)
+            sq1(0, 1, 1)
+            affine(0, 0, 1, "act")
+            turn_x(1, 0)
+            copy_x(1, 0, "dve")
+            turn_x(1, 2)
+            copy_x(1, 2, "act")
+            mm1(0, 1, 0)
+            affine(0, 0, 0, "act")
+            sq1(0, 1, 0)
+            affine(0, 0, 2, "dve")
+            turn_x(1, 3)
+            mm1(0, 1, 2)
+            sq1(0, 1, 2)
+            mm1(0, 1, 3)
+            copy_x(1, 3, "dve")
+            affine(0, 0, 3, "dve")
+            sq1(0, 1, 3)
+            sq2(0, 1, 0, "act")
+            sq2(0, 1, 1, "act")
+            quant_x(1, 1)
+            affine(0, 1, 1, "act")
             perm_perc_scales(1)
-            weave_e(0, 1)
-            sq2(1, 0, 0)
-            sq1(1, 0, 2)
-            mm1(1, 0, 3)
+            affine(0, 1, 2, "act")
+            weave_e(0, 0, "dve")
+            quant_x(1, 0)
+            affine(0, 1, 0, "dve")
+            quant_e(0, 0)
+            affine(0, 1, 3, "dve")
+            mm1(1, 1, 3)
+            sq1(1, 1, 3)
+            mm1(1, 0, 1)
+            sq1(1, 0, 1)
+            weave_e(0, 1, "dve")
             quant_e(0, 1)
+            mm1(1, 0, 3)
             sq1(1, 0, 3)
-            leave_pair(0, 0)
+            mm1(1, 0, 2)
+            sq1(1, 0, 2)
             sq2(1, 0, 1, "dve")
-            aff(1, 0, 0, 1)
-            leave_pair(0, 1)
-            low1(0, 0)
-            aff(1, 0, 2, 3)
-            leave_pair(0, 2)
+            mm1(1, 0, 0)
+            sq1(1, 0, 0)
+            mm2(0, 6)
+            leave(0, 6, "act")
+            mm2(0, 5)
+            leave(0, 5, "act")
+            sq2(1, 0, 0, "act")
+            mm2(0, 2)
+            leave(0, 2, "dve")
+            mm2(0, 1)
+            affine(1, 0, 2, "dve")
+            mm2(0, 4)
+            leave(0, 4, "act")
+            mm2(0, 0)
+            leave(0, 0, "act")
+            affine(1, 0, 1, "act")
+            leave(0, 1, "dve")
             low1(0, 1)
-            low2(0, 1)
-            weave_e(1, 0)
-            leave_pair(0, 3)
+            mm2(0, 3)
+            mm1(1, 1, 2)
+            sq1(1, 1, 2)
             low1(0, 2)
+            low1(0, 0)
+            mm2(0, 7)
+            low2(0, 1)
+            leave(0, 7, "act")
             low2(0, 2)
+            mm1(1, 1, 0)
+            leave(0, 3, "act")
             low1(0, 3)
-            m1(1, 1, 0, 1)
-            sq2(1, 1, 0)
-            quant_e(1, 0)
+            affine(1, 0, 3, "act")
             low2(0, 3)
-            low4(0)
-            m1(1, 1, 2, 3)
-            sq2(1, 1, 1, "dve")
-            turn_pair(0, 0)
-            expos(0, 0)
-            aff(1, 1, 0, 1)
-            turn_pair(0, 1)
-            sums(0, 0, 0, 2)
-            expos(0, 1)
-            aff(1, 1, 2, 3)
-            weave_e(1, 1)
-            sums(0, 1, 0, 2)
-            sums_out(0, 0, 2)
+            low4(0, "dve")
+            mm1(1, 1, 1)
+            sq1(1, 1, 1)
+            sq1(1, 1, 0)
+            sq2(1, 1, 1, "act")
+            heat(2, 5, "on")
+            heat(2, 0, "on")
+            sq2(1, 1, 0, "act")
+            affine(1, 1, 3, "act")
+            affine(1, 1, 1, "act")
+            turn_d(0, 0, 0)
+            affine(1, 0, 0, "dve")
+            weave_e(1, 0, "dve")
+            turn_d(0, 1, 1)
+            turn_d(0, 1, 0)
+            turn_d(0, 2, 0)
+            expo(0, 0, 0)
+            turn_d(0, 0, 1)
+            expo(0, 1, 0)
+            affine(1, 1, 2, "dve")
+            affine(1, 1, 0, "dve")
+            expo(0, 1, 1)
+            quant_e(1, 0)
+            expo(0, 0, 1)
+            weave_e(1, 1, "dve")
             quant_e(1, 1)
-            invert_a(0, 0, 2)
-            invert_c(0, 0)
-            mm2(1, 0)
-            mm2(1, 4)
-            leave(1, 0)
-            leave(1, 4)
             mm2(1, 1)
-            invert_e(0, 0, 2)
-            turn_inv(0, 0, 2)
+            leave(1, 1, "act")
+            fold1(0, 1)
+            mm2(1, 0)
+            leave(1, 0, "act")
+            fold1(0, 0)
+            fold2(0, 1)
+            fold2(0, 0)
+            fold3(0, 1, 0)
+            fold3(0, 0, 0)
+            invert_a(0, 0, 2)
+            mm2(1, 7)
+            leave(1, 7, "dve")
+            expo(0, 2, 0)
             mm2(1, 5)
-            leave(1, 1)
-            leave(1, 5)
+            mm2(1, 4)
+            invert_c(0, 0)
+            leave(1, 4, "act")
             low1(1, 0)
-            turn_pair(0, 2)
-            shares(0, 0)
-            result(0, 0, "pool")
-            leave_pair(1, 2)
+            mm2(1, 3)
+            leave(1, 5, "act")
             low1(1, 1)
-            low2(1, 1)
-            leave_pair(1, 3)
-            expos(0, 2)
-            turn_pair(0, 3)
-            sums(0, 2, 2, 2)
-            expos(0, 3)
-            sums(0, 3, 2, 2)
-            sums_out(0, 2, 2)
-            shares(0, 1)
-            result(0, 1, "pool")
-            low1(1, 2)
-            low2(1, 2)
+            leave(1, 3, "act")
             low1(1, 3)
+            turn_d(0, 2, 1)
+            expo(0, 2, 1)
+            fold1(0, 2)
+            mm2(1, 2)
+            leave(1, 2, "act")
+            mm2(1, 6)
+            turn_d(0, 3, 0)
+            low2(1, 1)
+            leave(1, 6, "act")
+            low1(1, 2)
+            fold2(0, 2)
+            low2(1, 2)
+            expo(0, 3, 0)
+            invert_e(0, 0, 2)
+            turn_d(0, 3, 1)
+            expo(0, 3, 1)
             low2(1, 3)
-            low4(1)
-            turn_pair(1, 0)
-            expos(1, 0)
-            turn_pair(1, 1)
+            fold1(0, 3)
+            share(0, 1, 1)
+            fold2(0, 3)
+            share(0, 1, 0)
+            low4(1, "act")
+            turn_d(1, 1, 1)
+            result(0, 1, "act")
+            fold3(0, 3, 2)
+            fold3(0, 2, 2)
+            share(0, 0, 0)
+            heat(2, 4, "on")
+            turn_d(1, 0, 1)
             invert_a(0, 2, 2)
+            share(0, 0, 1)
+            expo(1, 1, 1)
+            result(0, 0, "act")
             invert_c(0, 2)
             invert_e(0, 2, 2)
-            sums(1, 0, 0, 2)
-            turn_inv(0, 2, 2)
-            expos(1, 1)
-            shares(0, 2)
-            result(0, 2, "act")
-            turn_pair(1, 2)
-            sums(1, 1, 0, 2)
-            sums_out(1, 0, 2)
-            expos(1, 2)
-            turn_pair(1, 3)
-            shares(0, 3)
-            result(0, 3, "pool")
-            invert_a(1, 0, 2)
-            invert_c(1, 0)
-            invert_e(1, 0, 2)
-            turn_inv(1, 0, 2)
-            sums(1, 2, 2, 2)
-            expos(1, 3)
-            sums(1, 3, 2, 2)
-            sums_out(1, 2, 2)
-            weave_y(0, 0, "act")
-            shares(1, 0)
-            result(1, 0, "pool")
+            share(0, 2, 1)
+            share(0, 2, 0)
+            heat(2, 9, "on")
+            share(0, 3, 0)
+            expo(1, 0, 1)
+            share(0, 3, 1)
+            turn_d(1, 1, 0)
+            turn_d(1, 0, 0)
+            expo(1, 1, 0)
+            expo(1, 0, 0)
+            turn_d(1, 2, 1)
+            result(0, 2, "dve")
+            fold1(1, 1)
+            fold1(1, 0)
+            result(0, 3, "act")
             weave_y(0, 1, "act")
+            fold2(1, 1)
+            expo(1, 2, 1)
+            fold2(1, 0)
+            fold3(1, 1, 0)
+            turn_d(1, 2, 0)
+            expo(1, 2, 0)
+            turn_d(1, 3, 0)
+            fold3(1, 0, 0)
+            invert_a(1, 0, 2)
+            quant_y(0, 1)
+            invert_c(1, 0)
+            fold1(1, 2)
+            turn_d(1, 3, 1)
+            invert_e(1, 0, 2)
+            fold2(1, 2)
+            share(1, 0, 1)
+            share(1, 0, 0)
+            weave_y(0, 2, "act")
+            expo(1, 3, 0)
+            expo(1, 3, 1)
+            fold1(1, 3)
+            share(1, 1, 0)
+            fold2(1, 3)
+            share(1, 1, 1)
+            fold3(1, 3, 2)
+            result(1, 0, "act")
+            fold3(1, 2, 2)
+            weave_y(0, 0, "act")
+            result(1, 1, "act")
+            weave_y(0, 3, "act")
             invert_a(1, 2, 2)
             invert_c(1, 2)
             invert_e(1, 2, 2)
-            turn_inv(1, 2, 2)
-            shares(1, 1)
-            result(1, 1, "act")
-            quant_y(0, 0)
-            quant_y(0, 1)
-            weave_y(0, 2, "act")
-            shares(1, 2)
-            result(1, 2, "act")
-            weave_y(0, 3, "dve")
-            shares(1, 3)
+            share(1, 2, 1)
+            share(1, 3, 1)
+            share(1, 3, 0)
             result(1, 3, "act")
+            share(1, 2, 0)
+            result(1, 2, "dve")
+            weave_y(1, 0, "act")
+            quant_y(0, 0)
+            heat(2, 7, "on")
             quant_y(0, 2)
             quant_y(0, 3)
-            weave_y(1, 0, "dve")
-            weave_y(1, 1, "act")
-            weave_y(1, 2, "dve")
+            weave_y(1, 3, "dve")
+            heat(2, 6, "on")
+            weave_y(1, 1, "dve")
             quant_y(1, 0)
-            weave_y(1, 3, "act")
-            quant_y(1, 2)
             quant_y(1, 1)
+            weave_y(1, 2, "act")
+            quant_y(1, 2)
             quant_y(1, 3)

@@ -32,7 +32,8 @@ def tile_bprexcessdelaylogitroutesplit_x2_kernel(
         five = ctx.enter_context(tc.tile_pool(name="five", bufs=5))
         four = ctx.enter_context(tc.tile_pool(name="four", bufs=4))
         three = ctx.enter_context(tc.tile_pool(name="three", bufs=3))
-        turn = ctx.enter_context(tc.psum_pool(name="turn", bufs=4))
+        turn = ctx.enter_context(tc.psum_pool(name="turn", bufs=3))
+        spare = ctx.enter_context(tc.psum_pool(name="spare", bufs=1))
         mm = ctx.enter_context(tc.psum_pool(name="mm", bufs=4))
 
         x_rows = x.rearrange("(g m t) k -> g m t k", g=2, t=4)
@@ -59,26 +60,25 @@ def tile_bprexcessdelaylogitroutesplit_x2_kernel(
         ident = keep.tile([P, P], F32)
         make_identity(nc, ident[:])
         blank = keep.tile([P, HALF], BF16, align_bytes=64)
-        nc.vector.memset(blank[:], 0.0)
         nc.vector.memset(raw_s["dlt"][:].rearrange("p g n -> p (g n)").bitcast(I32), 0)
+        nc.vector.memset(blank[:], 0.0)
         nc.vector.memset(raw_s["perc"][:].rearrange("p g n -> p (g n)").bitcast(I32), 0)
         load_words("dlt", dlt_words, 0)
-        load_words("dlt", dlt_words, 1)
-        for key, src in (("cap", cap), ("f0", f0)):
-            vec[key] = keep.tile([P, 2, 4], BF16, name="v_" + key)
-            nc.scalar.dma_start(out=vec[key][:], in_=src.rearrange("(h p t) -> p h t", h=2, t=4))
+        for tt in (0, 2):
+            nc.sync.dma_start(out=x_sb[0][:, tt : tt + 2, :], in_=x_rows[0, :, tt : tt + 2, :])
+            if tt == 0:
+                load_words("dlt", dlt_words, 1)
         load_scales("dlt", dlt_scales, nc.scalar)
-        for t in range(4):
-            nc.sync.dma_start(out=x_sb[0][:, t, :], in_=x_rows[0, :, t, :])
-        vec["t0"] = keep.tile([P, 2, 4], BF16, name="v_t0")
-        nc.gpsimd.dma_start(out=vec["t0"][:], in_=t0.rearrange("(h p t) -> p h t", h=2, t=4))
+        for key, src in (("cap", cap), ("f0", f0), ("t0", t0)):
+            vec[key] = keep.tile([P, 2, 4], BF16, name="v_" + key)
+            nc.gpsimd.dma_start(out=vec[key][:], in_=src.rearrange("(h p t) -> p h t", h=2, t=4))
         c0_bf = keep.tile([P, R], BF16)
         nc.gpsimd.dma_start(out=c0_bf[:], in_=c0.rearrange("(o r) -> o r", r=R))
         load_scales("perc", perc_scales, nc.gpsimd)
         load_words("perc", perc_words, 0)
         load_words("perc", perc_words, 1)
-        for t in range(4):
-            nc.sync.dma_start(out=x_sb[1][:, t, :], in_=x_rows[1, :, t, :])
+        for tt in (0, 2):
+            nc.sync.dma_start(out=x_sb[1][:, tt : tt + 2, :], in_=x_rows[1, :, tt : tt + 2, :])
 
         dw = keep.tile([P, 2, 2 * D], U8, align_bytes=64)
         ds = keep.tile([P, 2, D], U8, align_bytes=64)
@@ -91,6 +91,8 @@ def tile_bprexcessdelaylogitroutesplit_x2_kernel(
                     out=dw[:, g, 1024 * h : 1024 * (h + 1)].rearrange("p (t m b) -> p t m b", t=4, b=2),
                     in_=raw["dlt"][:, g, 1024 * h : 1024 * (h + 1)].rearrange("p (m t b) -> p t m b", t=4, b=2),
                 )
+
+        def perm_dlt_scales(h):
             for g in range(2):
                 nc.vector.tensor_copy(
                     out=ds[:, g, HALF * h : HALF * (h + 1)].rearrange("p (t m) -> p t m", t=4),
@@ -131,14 +133,14 @@ def tile_bprexcessdelaylogitroutesplit_x2_kernel(
 
         xg, xc, xs, ec, es, cc, negm, y, yw, ysc, q, e16, eg, low, bank, w, inv, inv_t, total, total_s, u, yb, acc, prod, prod2, rec, done_y, part = ({} for _ in range(28))
 
+        idle = spare.tile([P, HALF], F32, name="idle")
+
         def warm(n, k, eng):
             for _ in range(n if eng == "on" else 0):
-                idle = mm.tile([P, HALF], F32, name="acc")
                 nc.tensor.matmul(idle[:], blank[:, 0:P], blank[:], start=True, stop=True)
 
         def heat(n, k, eng):
             for _ in range(n if eng == "on" else 0):
-                idle = mm.tile([P, HALF], F32, name="acc")
                 nc.tensor.matmul_mx(
                     out=idle[:],
                     lhsT=dw[:, 0, 0:256].bitcast(FP4X4),
@@ -293,26 +295,19 @@ def tile_bprexcessdelaylogitroutesplit_x2_kernel(
 
         def expo(g, t, hf):
             if (g, t) not in w:
-                w[g, t] = five.tile([P, R, P], F32, name="w")
+                w[g, t] = five.tile([P, P, R], F32, name="w")
             nc.scalar.activation(
-                out=w[g, t][:, 4 * hf : 4 * hf + 4, :], in_=bank[g, t, hf][:], func=ACT.Exp, scale=-1.0
+                out=w[g, t][:, :, 4 * hf : 4 * hf + 4],
+                in_=bank[g, t, hf][:].rearrange("m r o -> m o r"),
+                func=ACT.Exp, scale=-1.0,
             )
 
-        def fold1(g, t):
-            part[g, t] = two.tile([P, 6, P], F32, name="part")
-            nc.vector.tensor_tensor(
-                out=part[g, t][:, 0:4, :], in0=w[g, t][:, 0:4, :], in1=w[g, t][:, 4:8, :], op=ALU.add
-            )
-
-        def fold2(g, t):
-            pt = part[g, t]
-            nc.vector.tensor_tensor(out=pt[:, 4:6, :], in0=pt[:, 0:2, :], in1=pt[:, 2:4, :], op=ALU.add)
-
-        def fold3(g, t, t0_):
+        def fsum(g, t, t0_):
             if (g, t0_) not in total_s:
                 total_s[g, t0_] = two.tile([P, 2, P], F32, name="total_s")
-            pt = part[g, t]
-            nc.vector.tensor_tensor(out=total_s[g, t0_][:, t - t0_, :], in0=pt[:, 4, :], in1=pt[:, 5, :], op=ALU.add)
+            nc.vector.tensor_reduce(
+                out=total_s[g, t0_][:, t - t0_, :], in_=w[g, t][:], axis=mybir.AxisListType.X, op=ALU.add
+            )
 
         def mul(out, in0, in1):
             nc.vector.tensor_tensor(out=out, in0=in0, in1=in1, op=ALU.mult)
@@ -347,32 +342,24 @@ def tile_bprexcessdelaylogitroutesplit_x2_kernel(
                 mul(iv[:, 0, :], rec[g, t0_][:], s[:, 1, :])
                 mul(iv[:, 1, :], rec[g, t0_][:], s[:, 0, :])
 
-        def share(g, t, hf):
-            if (g, t) not in u:
-                u[g, t] = two.tile([P, P, R], F32, name="u")
-            nc.vector.tensor_tensor(
-                out=u[g, t][:, :, 4 * hf : 4 * hf + 4],
-                in0=w[g, t][:, 4 * hf : 4 * hf + 4, :].rearrange("m r o -> m o r"),
-                in1=inv[g, 2 * (t // 2)][:, t % 2, :].unsqueeze(2).to_broadcast([P, P, 4]),
-                op=ALU.mult,
+        def share(g, t):
+            mul(
+                w[g, t][:], w[g, t][:],
+                inv[g, 2 * (t // 2)][:, t % 2, :].unsqueeze(2).to_broadcast([P, P, R]),
             )
 
-        def result(g, t, eng):
+        def result(g, t, part, eng):
             if g not in y:
                 y[g] = two.tile([P, 4, D], F32, name="y")
-            src = u[g, t][:].rearrange("m o r -> m (o r)")
+            cols = (slice(0, HALF), slice(HALF, D), slice(0, D))[part]
+            out = y[g][:, t, cols]
+            src = w[g, t][:].rearrange("m o r -> m (o r)")[:, cols]
             if eng == "act":
-                nc.scalar.activation(out=y[g][:, t, :], in_=src, func=ACT.Copy, scale=8.0, bias=-1.0)
-            elif eng == "pool":
-                nc.gpsimd.tensor_scalar(
-                    out=y[g][:, t, :], in0=src, scalar1=8.0, scalar2=-1.0, op0=ALU.mult, op1=ALU.add
-                )
+                nc.scalar.activation(out=out, in_=src, func=ACT.Copy, scale=8.0, bias=-1.0)
             else:
-                nc.vector.tensor_scalar(
-                    out=y[g][:, t, :], in0=src, scalar1=8.0, scalar2=-1.0, op0=ALU.mult, op1=ALU.add
-                )
+                nc.vector.tensor_scalar(out=out, in0=src, scalar1=8.0, scalar2=-1.0, op0=ALU.mult, op1=ALU.add)
             nc.sync.dma_start(
-                out=out_0.rearrange("(g m t) p -> g m t p", g=2, t=4)[g, :, t, :], in_=y[g][:, t, :]
+                out=out_0.rearrange("(g m t) p -> g m t p", g=2, t=4)[g, :, t, cols], in_=out
             )
 
         def weave_y(g, c, eng):
@@ -410,258 +397,242 @@ def tile_bprexcessdelaylogitroutesplit_x2_kernel(
 
 
         with tc.manual_schedule():
-            perm_dlt(0)
+            perm_dlt_scales(0)
             warm(6, 0, "on")
-            warm(0, 1, "on")
             turn_x(0, 0)
             copy_x(0, 0, "act")
-            perm_dlt(1)
             turn_x(0, 1)
+            turn_x(0, 3)
+            perm_dlt(0)
             copy_x(0, 1, "act")
             turn_x(0, 2)
+            copy_x(0, 3, "act")
             copy_x(0, 2, "act")
-            turn_x(0, 3)
-            copy_x(0, 3, "dve")
-            quant_x(0, 1)
-            turn_x(1, 1)
-            quant_x(0, 0)
+            perm_dlt_scales(1)
             constants()
-            perm_perc_words(1)
-            copy_x(1, 1, "act")
-            mm1(0, 0, 2)
-            perm_perc_words(0)
+            turn_x(1, 1)
+            perm_dlt(1)
+            quant_x(0, 0)
+            quant_x(0, 1)
             mm1(0, 0, 1)
-            sq1(0, 0, 2)
-            sq1(0, 0, 1)
-            mm1(0, 0, 0)
-            mm1(0, 0, 3)
-            perm_perc_scales(0)
-            sq1(0, 0, 0)
-            sq2(0, 0, 0, "dve")
-            sq1(0, 0, 3)
-            sq2(0, 0, 1, "dve")
-            mm1(0, 1, 1)
-            sq1(0, 1, 1)
-            affine(0, 0, 1, "act")
-            turn_x(1, 0)
-            copy_x(1, 0, "dve")
-            turn_x(1, 2)
-            copy_x(1, 2, "act")
-            mm1(0, 1, 0)
-            affine(0, 0, 0, "act")
-            sq1(0, 1, 0)
-            affine(0, 0, 2, "dve")
             turn_x(1, 3)
-            mm1(0, 1, 2)
-            sq1(0, 1, 2)
-            mm1(0, 1, 3)
-            copy_x(1, 3, "dve")
-            affine(0, 0, 3, "dve")
-            sq1(0, 1, 3)
-            sq2(0, 1, 0, "act")
-            sq2(0, 1, 1, "act")
-            quant_x(1, 1)
-            affine(0, 1, 1, "act")
+            perm_perc_words(0)
+            copy_x(1, 1, "dve")
+            sq1(0, 0, 1)
+            copy_x(1, 3, "act")
+            perm_perc_words(1)
+            mm1(0, 0, 0)
+            mm1(0, 1, 1)
+            mm1(0, 1, 0)
+            mm1(0, 0, 3)
+            sq1(0, 0, 0)
+            sq1(0, 1, 1)
+            turn_x(1, 0)
+            turn_x(1, 2)
+            sq1(0, 1, 0)
+            perm_perc_scales(0)
+            sq2(0, 0, 0, "act")
+            mm1(0, 0, 2)
             perm_perc_scales(1)
-            affine(0, 1, 2, "act")
-            weave_e(0, 0, "dve")
+            sq1(0, 0, 3)
+            mm1(0, 1, 3)
+            copy_x(1, 2, "act")
+            sq2(0, 1, 0, "dve")
+            sq1(0, 0, 2)
+            sq1(0, 1, 3)
+            copy_x(1, 0, "dve")
+            affine(0, 0, 1, "dve")
+            affine(0, 0, 0, "dve")
+            affine(0, 1, 1, "dve")
+            mm1(0, 1, 2)
             quant_x(1, 0)
-            affine(0, 1, 0, "dve")
-            quant_e(0, 0)
-            affine(0, 1, 3, "dve")
-            mm1(1, 1, 3)
-            sq1(1, 1, 3)
+            sq1(0, 1, 2)
+            sq2(0, 0, 1, "dve")
+            quant_x(1, 1)
+            affine(0, 0, 3, "dve")
+            affine(0, 0, 2, "dve")
+            sq2(0, 1, 1, "act")
+            affine(0, 1, 2, "dve")
+            weave_e(0, 0, "dve")
+            affine(0, 1, 3, "act")
+            affine(0, 1, 0, "act")
             mm1(1, 0, 1)
             sq1(1, 0, 1)
             weave_e(0, 1, "dve")
-            quant_e(0, 1)
-            mm1(1, 0, 3)
-            sq1(1, 0, 3)
             mm1(1, 0, 2)
-            sq1(1, 0, 2)
-            sq2(1, 0, 1, "dve")
+            quant_e(0, 0)
+            quant_e(0, 1)
             mm1(1, 0, 0)
+            mm1(1, 1, 0)
+            sq1(1, 0, 2)
             sq1(1, 0, 0)
-            mm2(0, 6)
-            leave(0, 6, "act")
-            mm2(0, 5)
-            leave(0, 5, "act")
-            sq2(1, 0, 0, "act")
-            mm2(0, 2)
-            leave(0, 2, "dve")
-            mm2(0, 1)
-            affine(1, 0, 2, "dve")
+            mm1(1, 1, 3)
+            mm1(1, 0, 3)
+            sq1(1, 1, 0)
             mm2(0, 4)
-            leave(0, 4, "act")
+            mm2(0, 6)
+            sq1(1, 0, 3)
+            sq1(1, 1, 3)
+            mm2(0, 2)
             mm2(0, 0)
-            leave(0, 0, "act")
+            sq2(1, 0, 0, "act")
+            sq2(1, 0, 1, "dve")
+            affine(1, 0, 2, "dve")
+            leave(0, 4, "act")
+            affine(1, 0, 3, "dve")
             affine(1, 0, 1, "act")
-            leave(0, 1, "dve")
-            low1(0, 1)
+            leave(0, 2, "act")
+            leave(0, 6, "dve")
+            mm2(0, 1)
+            mm2(0, 5)
+            leave(0, 1, "act")
+            leave(0, 5, "act")
+            leave(0, 0, "dve")
             mm2(0, 3)
-            mm1(1, 1, 2)
-            sq1(1, 1, 2)
             low1(0, 2)
             low1(0, 0)
             mm2(0, 7)
+            low1(0, 1)
             low2(0, 1)
-            leave(0, 7, "act")
-            low2(0, 2)
-            mm1(1, 1, 0)
             leave(0, 3, "act")
+            leave(0, 7, "act")
+            mm1(1, 1, 2)
+            sq1(1, 1, 2)
             low1(0, 3)
-            affine(1, 0, 3, "act")
+            low2(0, 2)
+            mm1(1, 1, 1)
             low2(0, 3)
             low4(0, "dve")
-            mm1(1, 1, 1)
-            sq1(1, 1, 1)
-            sq1(1, 1, 0)
-            sq2(1, 1, 1, "act")
-            heat(2, 5, "on")
-            heat(2, 0, "on")
-            sq2(1, 1, 0, "act")
-            affine(1, 1, 3, "act")
-            affine(1, 1, 1, "act")
-            turn_d(0, 0, 0)
-            affine(1, 0, 0, "dve")
-            weave_e(1, 0, "dve")
-            turn_d(0, 1, 1)
             turn_d(0, 1, 0)
-            turn_d(0, 2, 0)
-            expo(0, 0, 0)
+            turn_d(0, 1, 1)
+            heat(1, 11, "on")
+            heat(1, 13, "on")
             turn_d(0, 0, 1)
+            sq1(1, 1, 1)
+            affine(1, 0, 0, "act")
+            sq2(1, 1, 0, "act")
+            weave_e(1, 0, "dve")
+            sq2(1, 1, 1, "act")
+            affine(1, 1, 1, "dve")
+            affine(1, 1, 3, "act")
+            affine(1, 1, 2, "act")
             expo(0, 1, 0)
-            affine(1, 1, 2, "dve")
+            turn_d(0, 0, 0)
             affine(1, 1, 0, "dve")
-            expo(0, 1, 1)
             quant_e(1, 0)
-            expo(0, 0, 1)
+            expo(0, 1, 1)
             weave_e(1, 1, "dve")
             quant_e(1, 1)
-            mm2(1, 1)
-            leave(1, 1, "act")
-            fold1(0, 1)
-            mm2(1, 0)
-            leave(1, 0, "act")
-            fold1(0, 0)
-            fold2(0, 1)
-            fold2(0, 0)
-            fold3(0, 1, 0)
-            fold3(0, 0, 0)
-            invert_a(0, 0, 2)
             mm2(1, 7)
-            leave(1, 7, "dve")
-            expo(0, 2, 0)
+            mm2(1, 3)
+            expo(0, 0, 1)
             mm2(1, 5)
+            expo(0, 0, 0)
+            fsum(0, 1, 0)
+            mm2(1, 1)
+            fsum(0, 0, 0)
+            leave(1, 7, "act")
+            invert_a(0, 0, 2)
+            mm2(1, 0)
+            leave(1, 3, "act")
+            leave(1, 5, "act")
             mm2(1, 4)
+            low1(1, 3)
             invert_c(0, 0)
+            leave(1, 1, "act")
+            low1(1, 1)
+            leave(1, 0, "act")
             leave(1, 4, "act")
             low1(1, 0)
-            mm2(1, 3)
-            leave(1, 5, "act")
-            low1(1, 1)
-            leave(1, 3, "act")
-            low1(1, 3)
-            turn_d(0, 2, 1)
-            expo(0, 2, 1)
-            fold1(0, 2)
-            mm2(1, 2)
-            leave(1, 2, "act")
             mm2(1, 6)
-            turn_d(0, 3, 0)
-            low2(1, 1)
+            mm2(1, 2)
+            turn_d(0, 2, 1)
             leave(1, 6, "act")
-            low1(1, 2)
-            fold2(0, 2)
-            low2(1, 2)
-            expo(0, 3, 0)
+            leave(1, 2, "act")
             invert_e(0, 0, 2)
-            turn_d(0, 3, 1)
-            expo(0, 3, 1)
+            low2(1, 1)
+            low1(1, 2)
+            turn_d(0, 3, 0)
+            low2(1, 2)
+            share(0, 1)
+            warm(0, 1, "on")
+            expo(0, 2, 1)
             low2(1, 3)
-            fold1(0, 3)
-            share(0, 1, 1)
-            fold2(0, 3)
-            share(0, 1, 0)
+            turn_d(0, 3, 1)
+            turn_d(0, 2, 0)
+            expo(0, 3, 0)
+            expo(0, 3, 1)
+            heat(1, 7, "on")
+            expo(0, 2, 0)
+            fsum(0, 2, 2)
+            fsum(0, 3, 2)
             low4(1, "act")
-            turn_d(1, 1, 1)
-            result(0, 1, "act")
-            fold3(0, 3, 2)
-            fold3(0, 2, 2)
-            share(0, 0, 0)
-            heat(2, 4, "on")
-            turn_d(1, 0, 1)
-            invert_a(0, 2, 2)
-            share(0, 0, 1)
-            expo(1, 1, 1)
-            result(0, 0, "act")
-            invert_c(0, 2)
-            invert_e(0, 2, 2)
-            share(0, 2, 1)
-            share(0, 2, 0)
-            heat(2, 9, "on")
-            share(0, 3, 0)
-            expo(1, 0, 1)
-            share(0, 3, 1)
+            heat(1, 16, "on")
             turn_d(1, 1, 0)
-            turn_d(1, 0, 0)
+            turn_d(1, 1, 1)
+            share(0, 0)
+            invert_a(0, 2, 2)
             expo(1, 1, 0)
-            expo(1, 0, 0)
-            turn_d(1, 2, 1)
-            result(0, 2, "dve")
-            fold1(1, 1)
-            fold1(1, 0)
-            result(0, 3, "act")
-            weave_y(0, 1, "act")
-            fold2(1, 1)
-            expo(1, 2, 1)
-            fold2(1, 0)
-            fold3(1, 1, 0)
+            turn_d(1, 0, 0)
+            invert_c(0, 2)
             turn_d(1, 2, 0)
-            expo(1, 2, 0)
-            turn_d(1, 3, 0)
-            fold3(1, 0, 0)
+            expo(1, 1, 1)
+            turn_d(1, 0, 1)
+            result(0, 1, 2, "act")
+            fsum(1, 1, 0)
+            invert_e(0, 2, 2)
+            expo(1, 0, 0)
+            result(0, 0, 2, "act")
+            share(0, 2)
+            expo(1, 0, 1)
+            fsum(1, 0, 0)
+            share(0, 3)
             invert_a(1, 0, 2)
-            quant_y(0, 1)
-            invert_c(1, 0)
-            fold1(1, 2)
+            expo(1, 2, 0)
+            turn_d(1, 2, 1)
+            result(0, 2, 2, "act")
+            expo(1, 2, 1)
+            turn_d(1, 3, 0)
             turn_d(1, 3, 1)
-            invert_e(1, 0, 2)
-            fold2(1, 2)
-            share(1, 0, 1)
-            share(1, 0, 0)
-            weave_y(0, 2, "act")
+            fsum(1, 2, 2)
             expo(1, 3, 0)
+            invert_c(1, 0)
+            result(0, 3, 2, "act")
             expo(1, 3, 1)
-            fold1(1, 3)
-            share(1, 1, 0)
-            fold2(1, 3)
-            share(1, 1, 1)
-            fold3(1, 3, 2)
-            result(1, 0, "act")
-            fold3(1, 2, 2)
-            weave_y(0, 0, "act")
-            result(1, 1, "act")
-            weave_y(0, 3, "act")
+            fsum(1, 3, 2)
+            weave_y(0, 2, "act")
+            invert_e(1, 0, 2)
             invert_a(1, 2, 2)
-            invert_c(1, 2)
-            invert_e(1, 2, 2)
-            share(1, 2, 1)
-            share(1, 3, 1)
-            share(1, 3, 0)
-            result(1, 3, "act")
-            share(1, 2, 0)
-            result(1, 2, "dve")
-            weave_y(1, 0, "act")
-            quant_y(0, 0)
-            heat(2, 7, "on")
             quant_y(0, 2)
+            share(1, 0)
+            weave_y(0, 1, "act")
+            heat(1, 0, "on")
+            quant_y(0, 1)
+            weave_y(0, 0, "act")
+            share(1, 1)
+            invert_c(1, 2)
+            quant_y(0, 0)
+            heat(1, 18, "on")
+            weave_y(0, 3, "act")
             quant_y(0, 3)
-            weave_y(1, 3, "dve")
-            heat(2, 6, "on")
+            heat(1, 12, "on")
+            heat(1, 21, "on")
+            result(1, 0, 2, "act")
+            invert_e(1, 2, 2)
+            result(1, 1, 2, "act")
+            share(1, 2)
+            result(1, 2, 0, "act")
+            share(1, 3)
+            heat(1, 15, "on")
+            result(1, 2, 1, "dve")
+            heat(1, 2, "on")
+            result(1, 3, 0, "dve")
             weave_y(1, 1, "dve")
-            quant_y(1, 0)
+            result(1, 3, 1, "act")
+            weave_y(1, 2, "dve")
+            weave_y(1, 0, "act")
+            weave_y(1, 3, "act")
             quant_y(1, 1)
-            weave_y(1, 2, "act")
             quant_y(1, 2)
+            quant_y(1, 0)
             quant_y(1, 3)

@@ -131,7 +131,13 @@ def tile_bprexcessdelaylogitroutesplit_x2_kernel(
             nc.vector.tensor_tensor(out=base4[:], in0=base2[:], in1=base2[:], op=ALU.mult)
             nc.vector.scalar_tensor_tensor(out=shift[:], in0=base4[:], scalar=-1.0, in1=gain[:], op0=ALU.mult, op1=ALU.mult)
 
-        xg, xc, xs, ec, es, cc, negm, y, yw, ysc, q, e16, eg, low, bank, w, inv, inv_t, total, total_s, u, yb, acc, prod, prod2, rec, done_y, part = ({} for _ in range(28))
+        CH = [[0,1],[2,3],[4,5,6,7]]
+        store = {}
+
+        def get(key, pool, shape, dtype, name, **kw):
+            if key not in store:
+                store[key] = pool.tile(shape, dtype, name=name, **kw)
+            return store[key]
 
         idle = spare.tile([P, HALF], F32, name="idle")
 
@@ -142,218 +148,221 @@ def tile_bprexcessdelaylogitroutesplit_x2_kernel(
         def heat(n, k, eng):
             for _ in range(n if eng == "on" else 0):
                 nc.tensor.matmul_mx(
-                    out=idle[:],
+                    out=idle[:, 0 : width(HOT)],
                     lhsT=dw[:, 0, 0:256].bitcast(FP4X4),
                     lhsT_scale=ds[:, 0, 0:P],
-                    rhs=xc[0][:, 0, :].bitcast(FP8X4),
-                    rhs_scale=xs[0][:, 0, :],
+                    rhs=store["xc", HOT][:, 0, :].bitcast(FP8X4),
+                    rhs_scale=store["xs", HOT][:, 0, :],
                     start=True,
                     stop=True,
                 )
 
-        def turn_x(g, t):
-            if g not in xg:
-                xg[g] = keep.tile([P, 2, HALF, 4], BF16, name="xg", align_bytes=64)
+        HOT = max(range(len(CH)), key=lambda c: (len(CH[c]), -c))
+
+        def where(slot):
+            for c, slots in enumerate(CH):
+                if slot in slots:
+                    return c, slots.index(slot)
+
+        def width(c):
+            return P * len(CH[c])
+
+        def turn_x(slot):
+            g, t = slot // 4, slot % 4
             words = x_sb[g][:].rearrange("p t k -> p (t k)").bitcast(F32)
-            bank[g, t] = turn.tile([P, 4, P], F32, name="bank")
+            bk = get(("xt", slot), turn, [P, 4, P], F32, "bank")
             for k in range(2):
                 for uu in range(2):
                     lo = HALF * t + 256 * k
-                    nc.tensor.transpose(bank[g, t][:, 2 * k + uu, :], words[:, lo + uu : lo + 256 : 2], ident[:])
+                    nc.tensor.transpose(bk[:, 2 * k + uu, :], words[:, lo + uu : lo + 256 : 2], ident[:])
 
-        def copy_x(g, t, eng):
-            out = xg[g][:].rearrange("p k n j -> p (k n j)").bitcast(F32)
-            out = out.rearrange("p (k n u) -> p k n u", k=2, u=2)[:, :, P * t : P * (t + 1), :]
-            src = bank[g, t][:].rearrange("p (k u) m -> p k m u", k=2)
+        def copy_x(slot, eng):
+            c, i = where(slot)
+            xg = get(("xg", c), two, [P, 2, width(c), 4], BF16, "xg", align_bytes=64)
+            out = xg[:].rearrange("p k n j -> p (k n j)").bitcast(F32)
+            out = out.rearrange("p (k n u) -> p k n u", k=2, u=2)[:, :, P * i : P * (i + 1), :]
+            src = store["xt", slot][:].rearrange("p (k u) m -> p k m u", k=2)
             if eng == "act":
                 nc.scalar.copy(out=out, in_=src)
             else:
                 nc.vector.tensor_copy(out=out, in_=src)
 
-        def quant_x(g, k):
-            if g not in xc:
-                xc[g] = two.tile([P, 2, HALF], U32, name="xc", align_bytes=64)
-                xs[g] = two.tile([P, 2, HALF], U8, name="xs", align_bytes=64)
+        def quant_x(c, k):
+            xc = get(("xc", c), two, [P, 2, width(c)], U32, "xc", align_bytes=64)
+            xs = get(("xs", c), two, [P, 2, width(c)], U8, "xs", align_bytes=64)
             nc.vector.quantize_mx(
-                out=xc[g][:, k, :].bitcast(FP8X4),
-                scales=xs[g][:, k, :],
-                in_=xg[g][:, k, :, :].rearrange("p n j -> p (n j)"),
+                out=xc[:, k, :].bitcast(FP8X4), scales=xs[:, k, :],
+                in_=store["xg", c][:, k, :, :].rearrange("p n j -> p (n j)"),
             )
 
-        def mm1(g, h, t):
-            if (g, h) not in q:
-                q[g, h] = two.tile([P, 4, HALF], F32, name="q")
-            a = acc[g, h, t] = mm.tile([P, HALF], F32, name="acc")
-            col = HALF * h + P * t
-            for k in range(2):
-                nc.tensor.matmul_mx(
-                    out=a[:],
-                    lhsT=dw[:, k, 2 * col : 2 * (col + P)].bitcast(FP4X4),
-                    lhsT_scale=ds[:, k, col : col + P],
-                    rhs=xc[g][:, k, :].bitcast(FP8X4),
-                    rhs_scale=xs[g][:, k, :],
-                    start=(k == 0),
-                    stop=(k == 1),
+        def product(out, weight, wscale, col, codes, scales, cols):
+            step = cols if cols == HALF else P
+            for n in range(0, cols, step):
+                for k in range(2):
+                    nc.tensor.matmul_mx(
+                        out=out[:, n : n + step],
+                        lhsT=weight[:, k, 2 * col : 2 * (col + P)].bitcast(FP4X4),
+                        lhsT_scale=wscale[:, k, col : col + P],
+                        rhs=codes[:, k, n : n + step].bitcast(FP8X4),
+                        rhs_scale=scales[:, k, n : n + step],
+                        start=(k == 0),
+                        stop=(k == 1),
+                    )
+
+        def mm1(c, h, i):
+            v = HALF // width(c)
+            a = get(("a1", c, h, i), mm, [P, v, width(c)], F32, "acc")
+            for j in range(v):
+                product(a[:, j, :], dw, ds, HALF * h + P * (v * i + j), store["xc", c], store["xs", c], width(c))
+
+        def sq1(c, h, i):
+            v = HALF // width(c)
+            q = get(("q", c, h), two, [P, 4, width(c)], F32, "q")
+            for j in range(v):
+                t = v * i + j
+                e = 4 * h + t
+                nc.scalar.activation(
+                    out=q[:, t, :], in_=store["a1", c, h, i][:, j, :], func=ACT.Square,
+                    scale=inv_cap[:, e : e + 1], bias=base[:, e : e + 1],
                 )
 
-        def sq1(g, h, t):
-            j = 4 * h + t
-            nc.scalar.activation(
-                out=q[g, h][:, t, :], in_=acc[g, h, t][:], func=ACT.Square,
-                scale=inv_cap[:, j : j + 1], bias=base[:, j : j + 1],
-            )
-
-        def sq2(g, h, i, eng):
-            v = q[g, h][:, 2 * i : 2 * i + 2, :]
+        def sq2(c, h, i, eng):
+            v = store["q", c, h][:, 2 * i : 2 * i + 2, :]
             if eng == "act":
                 nc.scalar.activation(out=v, in_=v, func=ACT.Square)
             else:
                 nc.vector.tensor_tensor(out=v, in0=v, in1=v, op=ALU.mult)
 
-        def affine(g, h, t, eng):
-            j = 4 * h + t
-            if (g, h) not in e16:
-                e16[g, h] = two.tile([P, 4, HALF], BF16, name="e16", align_bytes=64)
+        def affine(c, h, t, eng):
+            e = 4 * h + t
+            e16 = get(("e16", c, h), two, [P, 4, width(c)], BF16, "e16", align_bytes=64)
+            src = store["q", c, h][:, t, :]
             if eng == "act":
                 nc.scalar.activation(
-                    out=e16[g, h][:, t, :], in_=q[g, h][:, t, :], func=ACT.Identity,
-                    scale=gain[:, j : j + 1], bias=shift[:, j : j + 1],
+                    out=e16[:, t, :], in_=src, func=ACT.Identity, scale=gain[:, e : e + 1], bias=shift[:, e : e + 1]
                 )
             else:
                 nc.vector.tensor_scalar(
-                    out=e16[g, h][:, t, :], in0=q[g, h][:, t, :],
-                    scalar1=base4[:, j : j + 1], scalar2=gain[:, j : j + 1],
+                    out=e16[:, t, :], in0=src, scalar1=base4[:, e : e + 1], scalar2=gain[:, e : e + 1],
                     op0=ALU.subtract, op1=ALU.mult,
                 )
 
-        def weave_e(g, h, eng):
-            eg[g, h] = two.tile([P, HALF, 4], BF16, name="eg", align_bytes=64)
-            out = eg[g, h][:].rearrange("p (c i) t -> p c t i", i=4)
-            src = e16[g, h][:].rearrange("p t (c i) -> p c t i", i=4)
+        def weave_e(c, h, eng):
+            eg = get(("eg", c, h), two, [P, width(c), 4], BF16, "eg", align_bytes=64)
+            out = eg[:].rearrange("p (c i) t -> p c t i", i=4)
+            src = store["e16", c, h][:].rearrange("p t (c i) -> p c t i", i=4)
             if eng == "act":
                 nc.scalar.copy(out=out, in_=src)
             else:
                 nc.vector.tensor_copy(out=out, in_=src)
 
-        def quant_e(g, h):
-            if g not in ec:
-                ec[g] = two.tile([P, 2, HALF], U32, name="ec", align_bytes=64)
-                es[g] = two.tile([P, 2, HALF], U8, name="es", align_bytes=64)
+        def quant_e(c, h):
+            ec = get(("ec", c), two, [P, 2, width(c)], U32, "ec", align_bytes=64)
+            es = get(("es", c), two, [P, 2, width(c)], U8, "es", align_bytes=64)
             nc.vector.quantize_mx(
-                out=ec[g][:, h, :].bitcast(FP8X4), scales=es[g][:, h, :],
-                in_=eg[g, h][:].rearrange("p n j -> p (n j)"),
+                out=ec[:, h, :].bitcast(FP8X4), scales=es[:, h, :],
+                in_=store["eg", c, h][:].rearrange("p n j -> p (n j)"),
             )
 
-        def mm2(g, r):
-            a = acc[g, r] = mm.tile([P, HALF], F32, name="acc")
-            for k in range(2):
-                nc.tensor.matmul_mx(
-                    out=a[:],
-                    lhsT=pw[:, k, 256 * r : 256 * (r + 1)].bitcast(FP4X4),
-                    lhsT_scale=psc[:, k, P * r : P * (r + 1)],
-                    rhs=ec[g][:, k, :].bitcast(FP8X4),
-                    rhs_scale=es[g][:, k, :],
-                    start=(k == 0),
-                    stop=(k == 1),
-                )
+        def routes(c, i):
+            return (i,) if width(c) == HALF else (i, i + 4)
 
-        def leave(g, r, eng):
-            if g not in cc:
-                cc[g] = two.tile([P, R, HALF], F32, name="cc")
-            if eng == "act":
-                nc.scalar.activation(
-                    out=cc[g][:, r, :], in_=acc[g, r][:], func=ACT.Identity, scale=1.0, bias=c0_col[:, r : r + 1]
-                )
+        def mm2(c, i):
+            rs = routes(c, i)
+            a = get(("a2", c, i), mm, [P, len(rs), width(c)], F32, "acc")
+            for j, r in enumerate(rs):
+                product(a[:, j, :], pw, psc, P * r, store["ec", c], store["es", c], width(c))
+
+        def leave(c, i, eng):
+            cc = get(("cc", c), two, [P, R, width(c)], F32, "cc")
+            for j, r in enumerate(routes(c, i)):
+                if eng == "act":
+                    nc.scalar.activation(
+                        out=cc[:, r, :], in_=store["a2", c, i][:, j, :], func=ACT.Identity, scale=1.0,
+                        bias=c0_col[:, r : r + 1],
+                    )
+                else:
+                    nc.vector.tensor_scalar(
+                        out=cc[:, r, :], in0=store["a2", c, i][:, j, :], scalar1=c0_col[:, r : r + 1], scalar2=None,
+                        op0=ALU.add,
+                    )
+
+        def tmin(out, in0, in1):
+            nc.vector.tensor_tensor(out=out, in0=in0, in1=in1, op=ALU.min)
+
+        def low1(c, i):
+            cc = store["cc", c]
+            low = get(("low", c), keep, [P, 4, width(c)], F32, "low")
+            v = HALF // width(c)
+            tmin(low[:, v * i : v * (i + 1), :], cc[:, v * i : v * (i + 1), :], cc[:, v * i + 4 : v * (i + 1) + 4, :])
+
+        def low2(c, i):
+            low = store["low", c]
+            negm = get(("negm", c), two, [P, width(c)], F32, "negm")
+            if width(c) == HALF:
+                tmin(low[:, i, :] if i < 3 else negm[:], low[:, i - 1, :], low[:, i, :])
+            elif i == 1:
+                tmin(low[:, 0:2, :], low[:, 0:2, :], low[:, 2:4, :])
             else:
-                nc.vector.tensor_scalar(
-                    out=cc[g][:, r, :], in0=acc[g, r][:], scalar1=c0_col[:, r : r + 1], scalar2=None, op0=ALU.add
-                )
+                tmin(negm[:], low[:, 0, :], low[:, 1, :])
 
-        def low1(g, i):
-            if g not in low:
-                low[g] = keep.tile([P, 4, HALF], F32, name="low")
-                negm[g] = two.tile([P, HALF], F32, name="negm")
-            nc.vector.tensor_tensor(out=low[g][:, i, :], in0=cc[g][:, i, :], in1=cc[g][:, i + 4, :], op=ALU.min)
-
-        def low2(g, i):
-            nc.vector.tensor_tensor(
-                out=low[g][:, i, :] if i < 3 else negm[g][:], in0=low[g][:, i - 1, :], in1=low[g][:, i, :], op=ALU.min
-            )
-
-        def low4(g, eng):
+        def low4(c, eng):
+            negm = store["negm", c]
             if eng == "act":
-                nc.scalar.activation(out=negm[g][:], in_=negm[g][:], func=ACT.Copy, scale=-1.0)
+                nc.scalar.activation(out=negm[:], in_=negm[:], func=ACT.Copy, scale=-1.0)
             else:
-                nc.vector.tensor_scalar(out=negm[g][:], in0=negm[g][:], scalar1=-1.0, scalar2=None, op0=ALU.mult)
+                nc.vector.tensor_scalar(out=negm[:], in0=negm[:], scalar1=-1.0, scalar2=None, op0=ALU.mult)
 
-        def turn_d(g, t, hf):
-            cols = slice(P * t, P * (t + 1))
-            b = bank[g, t, hf] = turn.tile([P, 4, P], F32, name="bank")
-            for i in range(4):
-                nc.tensor.matmul(b[:, i, :], cc[g][:, 4 * hf + i, cols], ident[:], start=True, stop=False, is_transpose=True)
-                nc.tensor.matmul(b[:, i, :], negm[g][:, cols], ident[:], start=False, stop=True, is_transpose=True)
+        def turn_d(slot, hf):
+            c, i = where(slot)
+            cols = slice(P * i, P * (i + 1))
+            cc, negm = store["cc", c], store["negm", c]
+            b = get(("d", slot, hf), turn, [P, 4, P], F32, "bank")
+            for j in range(4):
+                nc.tensor.matmul(b[:, j, :], cc[:, 4 * hf + j, cols], ident[:], start=True, stop=False, is_transpose=True)
+                nc.tensor.matmul(b[:, j, :], negm[:, cols], ident[:], start=False, stop=True, is_transpose=True)
 
-        def expo(g, t, hf):
-            if (g, t) not in w:
-                w[g, t] = five.tile([P, P, R], F32, name="w")
+        def expo(slot, hf):
+            w = get(("w", slot), five, [P, P, R], F32, "w")
             nc.scalar.activation(
-                out=w[g, t][:, :, 4 * hf : 4 * hf + 4],
-                in_=bank[g, t, hf][:].rearrange("m r o -> m o r"),
+                out=w[:, :, 4 * hf : 4 * hf + 4], in_=store["d", slot, hf][:].rearrange("m r o -> m o r"),
                 func=ACT.Exp, scale=-1.0,
             )
 
-        def fsum(g, t, t0_):
-            if (g, t0_) not in total_s:
-                total_s[g, t0_] = two.tile([P, 2, P], F32, name="total_s")
+        def fsum(slot):
+            tot = get(("tot", slot // 2), two, [P, 2, P], F32, "total_s")
             nc.vector.tensor_reduce(
-                out=total_s[g, t0_][:, t - t0_, :], in_=w[g, t][:], axis=mybir.AxisListType.X, op=ALU.add
+                out=tot[:, slot % 2, :], in_=store["w", slot][:], axis=mybir.AxisListType.X, op=ALU.add
             )
 
         def mul(out, in0, in1):
             nc.vector.tensor_tensor(out=out, in0=in0, in1=in1, op=ALU.mult)
 
-        def invert_a(g, t0_, n):
-            s = total_s[g, t0_]
-            prod[g, t0_] = two.tile([P, 3, P], F32, name="prod")
-            if n == 4:
-                mul(prod[g, t0_][:, 0:2, :], s[:, 0:2, :], s[:, 2:4, :])
-            else:
-                mul(prod[g, t0_][:, 2, :], s[:, 0, :], s[:, 1, :])
+        def invert_a(p):
+            prod = get(("prod", p), two, [P, P], F32, "prod")
+            tot = store["tot", p]
+            mul(prod[:], tot[:, 0, :], tot[:, 1, :])
 
-        def invert_b(g, t0_):
-            mul(prod[g, t0_][:, 2, :], prod[g, t0_][:, 0, :], prod[g, t0_][:, 1, :])
+        def invert_c(p):
+            rec = get(("rec", p), two, [P, P], F32, "rec")
+            nc.vector.reciprocal(rec[:], store["prod", p][:])
 
-        def invert_c(g, t0_):
-            rec[g, t0_] = two.tile([P, P], F32, name="rec")
-            nc.vector.reciprocal(rec[g, t0_][:], prod[g, t0_][:, 2, :])
+        def invert_e(p):
+            inv = get(("inv", p), two, [P, 2, P], F32, "inv")
+            tot = store["tot", p]
+            mul(inv[:, 0, :], store["rec", p][:], tot[:, 1, :])
+            mul(inv[:, 1, :], store["rec", p][:], tot[:, 0, :])
 
-        def invert_d(g, t0_):
-            pr = prod2[g, t0_] = two.tile([P, 2, P], F32, name="prod2")
-            mul(pr[:, 0, :], rec[g, t0_][:], prod[g, t0_][:, 1, :])
-            mul(pr[:, 1, :], rec[g, t0_][:], prod[g, t0_][:, 0, :])
+        def share(slot):
+            w = store["w", slot]
+            mul(w[:], w[:], store["inv", slot // 2][:, slot % 2, :].unsqueeze(2).to_broadcast([P, P, R]))
 
-        def invert_e(g, t0_, n):
-            s = total_s[g, t0_]
-            iv = inv[g, t0_] = two.tile([P, n, P], F32, name="inv%d" % n)
-            if n == 4:
-                mul(iv[:, 0:2, :], prod2[g, t0_][:], s[:, 2:4, :])
-                mul(iv[:, 2:4, :], prod2[g, t0_][:], s[:, 0:2, :])
-            else:
-                mul(iv[:, 0, :], rec[g, t0_][:], s[:, 1, :])
-                mul(iv[:, 1, :], rec[g, t0_][:], s[:, 0, :])
-
-        def share(g, t):
-            mul(
-                w[g, t][:], w[g, t][:],
-                inv[g, 2 * (t // 2)][:, t % 2, :].unsqueeze(2).to_broadcast([P, P, R]),
-            )
-
-        def result(g, t, part, eng):
-            if g not in y:
-                y[g] = two.tile([P, 4, D], F32, name="y")
+        def result(slot, part, eng):
+            g, t = slot // 4, slot % 4
+            y = get(("y", g), two, [P, 4, D], F32, "y")
             cols = (slice(0, HALF), slice(HALF, D), slice(0, D))[part]
-            out = y[g][:, t, cols]
-            src = w[g, t][:].rearrange("m o r -> m (o r)")[:, cols]
+            out = y[:, t, cols]
+            src = store["w", slot][:].rearrange("m o r -> m (o r)")[:, cols]
             if eng == "act":
                 nc.scalar.activation(out=out, in_=src, func=ACT.Copy, scale=8.0, bias=-1.0)
             else:
@@ -363,276 +372,288 @@ def tile_bprexcessdelaylogitroutesplit_x2_kernel(
             )
 
         def weave_y(g, c, eng):
-            if g not in yw:
-                yw[g] = two.tile([P, D], U32, name="yw", align_bytes=64)
-                ysc[g] = two.tile([P, D], U8, name="ysc", align_bytes=64)
-                nc.gpsimd.memset(ysc[g][:].bitcast(I32), 0)
-            yb[g, c] = four.tile([P, 256, 4], BF16, name="yb", align_bytes=64)
+            if ("yw", g) not in store:
+                get(("yw", g), two, [P, D], U32, "yw", align_bytes=64)
+                ysc = get(("ysc", g), two, [P, D], U8, "ysc", align_bytes=64)
+                nc.gpsimd.memset(ysc[:].bitcast(I32), 0)
+            yb = get(("yb", g, c), four, [P, 256, 4], BF16, "yb", align_bytes=64)
             cols = slice(256 * c, 256 * (c + 1))
-            out = yb[g, c][:].rearrange("p (c i) t -> p c t i", i=4)
-            src = y[g][:, :, cols].rearrange("p t (c i) -> p c t i", i=4)
+            out = yb[:].rearrange("p (c i) t -> p c t i", i=4)
+            src = store["y", g][:, :, cols].rearrange("p t (c i) -> p c t i", i=4)
             if eng == "act":
                 nc.scalar.copy(out=out, in_=src)
-            elif eng == "pool":
-                nc.gpsimd.tensor_scalar(out=out, in0=src, scalar1=1.0, scalar2=0.0, op0=ALU.mult, op1=ALU.add)
             else:
                 nc.vector.tensor_copy(out=out, in_=src)
 
         def quant_y(g, c):
+            yw, ysc = store["yw", g], store["ysc", g]
             cols = slice(256 * c, 256 * (c + 1))
             nc.vector.quantize_mx(
-                out=yw[g][:, cols].bitcast(FP8X4), scales=ysc[g][:, cols],
-                in_=yb[g, c][:].rearrange("p n j -> p (n j)"),
+                out=yw[:, cols].bitcast(FP8X4), scales=ysc[:, cols],
+                in_=store["yb", g, c][:].rearrange("p n j -> p (n j)"),
             )
             nc.sync.dma_start(
-                out=out_1[g].rearrange("m p t -> m (p t)").bitcast(I32)[:, cols], in_=yw[g][:, cols].bitcast(I32)
+                out=out_1[g].rearrange("m p t -> m (p t)").bitcast(I32)[:, cols], in_=yw[:, cols].bitcast(I32)
             )
-            done_y[g] = done_y.get(g, 0) + 1
-            if done_y[g] == 4:
+            store["done", g] = store.get(("done", g), 0) + 1
+            if store["done", g] == 4:
                 for qd in range(4):
                     nc.sync.dma_start(
                         out=out_2[g, 4 * qd : 4 * qd + 4, :].bitcast(I32),
-                        in_=ysc[g][32 * qd : 32 * qd + 4, :].bitcast(I32),
+                        in_=ysc[32 * qd : 32 * qd + 4, :].bitcast(I32),
                     )
 
 
         with tc.manual_schedule():
-            perm_dlt_scales(0)
             warm(6, 0, "on")
-            turn_x(0, 0)
-            copy_x(0, 0, "act")
-            turn_x(0, 1)
-            turn_x(0, 3)
             perm_dlt(0)
-            copy_x(0, 1, "act")
-            turn_x(0, 2)
-            copy_x(0, 3, "act")
-            copy_x(0, 2, "act")
+            perm_dlt_scales(0)
             perm_dlt_scales(1)
+            turn_x(0)
+            turn_x(1)
+            copy_x(0, "act")
+            turn_x(2)
             constants()
-            turn_x(1, 1)
-            perm_dlt(1)
+            copy_x(1, "act")
             quant_x(0, 0)
+            turn_x(3)
+            copy_x(2, "act")
             quant_x(0, 1)
-            mm1(0, 0, 1)
-            turn_x(1, 3)
-            perm_perc_words(0)
-            copy_x(1, 1, "dve")
-            sq1(0, 0, 1)
-            copy_x(1, 3, "act")
             perm_perc_words(1)
-            mm1(0, 0, 0)
-            mm1(0, 1, 1)
-            mm1(0, 1, 0)
-            mm1(0, 0, 3)
-            sq1(0, 0, 0)
-            sq1(0, 1, 1)
-            turn_x(1, 0)
-            turn_x(1, 2)
-            sq1(0, 1, 0)
-            perm_perc_scales(0)
-            sq2(0, 0, 0, "act")
-            mm1(0, 0, 2)
-            perm_perc_scales(1)
-            sq1(0, 0, 3)
-            mm1(0, 1, 3)
-            copy_x(1, 2, "act")
-            sq2(0, 1, 0, "dve")
-            sq1(0, 0, 2)
-            sq1(0, 1, 3)
-            copy_x(1, 0, "dve")
-            affine(0, 0, 1, "dve")
-            affine(0, 0, 0, "dve")
-            affine(0, 1, 1, "dve")
-            mm1(0, 1, 2)
-            quant_x(1, 0)
-            sq1(0, 1, 2)
-            sq2(0, 0, 1, "dve")
+            perm_dlt(1)
+            copy_x(3, "act")
             quant_x(1, 1)
+            mm1(0, 0, 1)
+            perm_perc_scales(1)
+            perm_perc_scales(0)
+            sq1(0, 0, 1)
+            sq2(0, 0, 1, "act")
+            perm_perc_words(0)
             affine(0, 0, 3, "dve")
+            quant_x(1, 0)
             affine(0, 0, 2, "dve")
-            sq2(0, 1, 1, "act")
+            mm1(0, 0, 0)
+            sq1(0, 0, 0)
+            turn_x(4)
+            turn_x(6)
+            mm1(0, 1, 1)
+            copy_x(6, "dve")
+            copy_x(4, "act")
+            sq2(0, 0, 0, "act")
+            mm1(0, 1, 0)
+            sq1(0, 1, 1)
+            sq2(0, 1, 1, "dve")
+            sq1(0, 1, 0)
+            sq2(0, 1, 0, "dve")
             affine(0, 1, 2, "dve")
+            affine(0, 1, 3, "dve")
+            turn_x(7)
+            affine(0, 1, 0, "dve")
+            affine(0, 0, 1, "act")
+            affine(0, 0, 0, "act")
             weave_e(0, 0, "dve")
-            affine(0, 1, 3, "act")
-            affine(0, 1, 0, "act")
+            copy_x(7, "dve")
+            turn_x(5)
+            copy_x(5, "act")
+            affine(0, 1, 1, "act")
+            mm1(1, 1, 0)
             mm1(1, 0, 1)
+            sq1(1, 1, 0)
             sq1(1, 0, 1)
             weave_e(0, 1, "dve")
-            mm1(1, 0, 2)
             quant_e(0, 0)
             quant_e(0, 1)
-            mm1(1, 0, 0)
-            mm1(1, 1, 0)
-            sq1(1, 0, 2)
-            sq1(1, 0, 0)
-            mm1(1, 1, 3)
-            mm1(1, 0, 3)
-            sq1(1, 1, 0)
-            mm2(0, 4)
-            mm2(0, 6)
-            sq1(1, 0, 3)
-            sq1(1, 1, 3)
-            mm2(0, 2)
-            mm2(0, 0)
-            sq2(1, 0, 0, "act")
+            quant_x(2, 0)
+            quant_x(2, 1)
             sq2(1, 0, 1, "dve")
-            affine(1, 0, 2, "dve")
-            leave(0, 4, "act")
-            affine(1, 0, 3, "dve")
-            affine(1, 0, 1, "act")
-            leave(0, 2, "act")
-            leave(0, 6, "dve")
-            mm2(0, 1)
-            mm2(0, 5)
-            leave(0, 1, "act")
-            leave(0, 5, "act")
-            leave(0, 0, "dve")
-            mm2(0, 3)
-            low1(0, 2)
-            low1(0, 0)
-            mm2(0, 7)
-            low1(0, 1)
-            low2(0, 1)
-            leave(0, 3, "act")
-            leave(0, 7, "act")
-            mm1(1, 1, 2)
-            sq1(1, 1, 2)
-            low1(0, 3)
-            low2(0, 2)
             mm1(1, 1, 1)
-            low2(0, 3)
-            low4(0, "dve")
-            turn_d(0, 1, 0)
-            turn_d(0, 1, 1)
-            heat(1, 11, "on")
-            heat(1, 13, "on")
-            turn_d(0, 0, 1)
             sq1(1, 1, 1)
-            affine(1, 0, 0, "act")
             sq2(1, 1, 0, "act")
-            weave_e(1, 0, "dve")
-            sq2(1, 1, 1, "act")
             affine(1, 1, 1, "dve")
-            affine(1, 1, 3, "act")
+            mm1(1, 0, 0)
+            sq2(1, 1, 1, "act")
+            sq1(1, 0, 0)
             affine(1, 1, 2, "act")
-            expo(0, 1, 0)
-            turn_d(0, 0, 0)
-            affine(1, 1, 0, "dve")
-            quant_e(1, 0)
-            expo(0, 1, 1)
+            affine(1, 1, 0, "act")
+            mm2(0, 3)
+            sq2(1, 0, 0, "dve")
+            leave(0, 3, "act")
+            mm2(0, 2)
+            leave(0, 2, "act")
+            affine(1, 0, 2, "dve")
+            affine(1, 1, 3, "dve")
+            affine(1, 0, 3, "dve")
+            affine(1, 0, 0, "dve")
             weave_e(1, 1, "dve")
+            low1(0, 1)
+            mm1(2, 0, 2)
+            mm1(2, 0, 3)
+            affine(1, 0, 1, "act")
+            mm2(0, 0)
+            mm2(0, 1)
+            sq1(2, 0, 3)
+            sq1(2, 0, 2)
+            leave(0, 0, "act")
+            leave(0, 1, "act")
             quant_e(1, 1)
-            mm2(1, 7)
-            mm2(1, 3)
-            expo(0, 0, 1)
-            mm2(1, 5)
-            expo(0, 0, 0)
-            fsum(0, 1, 0)
-            mm2(1, 1)
-            fsum(0, 0, 0)
-            leave(1, 7, "act")
-            invert_a(0, 0, 2)
-            mm2(1, 0)
-            leave(1, 3, "act")
-            leave(1, 5, "act")
-            mm2(1, 4)
-            low1(1, 3)
-            invert_c(0, 0)
-            leave(1, 1, "act")
-            low1(1, 1)
-            leave(1, 0, "act")
-            leave(1, 4, "act")
-            low1(1, 0)
-            mm2(1, 6)
+            mm1(2, 0, 0)
+            sq1(2, 0, 0)
+            sq2(2, 0, 1, "dve")
+            low1(0, 0)
+            weave_e(1, 0, "dve")
+            affine(2, 0, 2, "dve")
+            mm1(2, 0, 1)
+            sq1(2, 0, 1)
+            low2(0, 1)
+            sq2(2, 0, 0, "dve")
+            quant_e(1, 0)
+            affine(2, 0, 3, "dve")
+            affine(2, 0, 0, "dve")
+            low2(0, 2)
+            affine(2, 0, 1, "dve")
+            mm1(2, 1, 3)
+            sq1(2, 1, 3)
+            mm1(2, 1, 2)
+            sq1(2, 1, 2)
+            mm1(2, 1, 0)
+            sq1(2, 1, 0)
+            mm1(2, 1, 1)
+            sq1(2, 1, 1)
+            sq2(2, 1, 1, "act")
+            sq2(2, 1, 0, "act")
+            low4(0, "act")
             mm2(1, 2)
-            turn_d(0, 2, 1)
-            leave(1, 6, "act")
-            leave(1, 2, "act")
-            invert_e(0, 0, 2)
+            affine(2, 1, 3, "dve")
+            weave_e(2, 0, "dve")
+            leave(1, 2, "dve")
+            affine(2, 1, 1, "act")
+            affine(2, 1, 0, "act")
+            affine(2, 1, 2, "act")
+            mm2(1, 0)
+            quant_e(2, 0)
+            turn_d(0, 1)
+            mm2(1, 1)
+            weave_e(2, 1, "dve")
+            leave(1, 0, "act")
+            leave(1, 1, "act")
+            low1(1, 0)
+            quant_e(2, 1)
+            turn_d(1, 0)
+            mm2(1, 3)
+            expo(0, 1)
+            leave(1, 3, "act")
+            low1(1, 1)
+            turn_d(0, 0)
+            turn_d(1, 1)
+            expo(0, 0)
+            fsum(0)
+            mm2(2, 5)
+            expo(1, 0)
             low2(1, 1)
-            low1(1, 2)
-            turn_d(0, 3, 0)
+            expo(1, 1)
+            fsum(1)
+            mm2(2, 1)
+            leave(2, 5, "act")
             low2(1, 2)
-            share(0, 1)
-            warm(0, 1, "on")
-            expo(0, 2, 1)
-            low2(1, 3)
-            turn_d(0, 3, 1)
-            turn_d(0, 2, 0)
-            expo(0, 3, 0)
-            expo(0, 3, 1)
-            heat(1, 7, "on")
-            expo(0, 2, 0)
-            fsum(0, 2, 2)
-            fsum(0, 3, 2)
+            leave(2, 1, "act")
+            mm2(2, 0)
+            invert_a(0)
+            mm2(2, 4)
+            low1(2, 1)
+            leave(2, 0, "act")
+            leave(2, 4, "act")
+            low1(2, 0)
+            invert_c(0)
+            low2(2, 1)
+            mm2(2, 3)
+            mm2(2, 7)
+            leave(2, 7, "act")
+            mm2(2, 6)
             low4(1, "act")
-            heat(1, 16, "on")
-            turn_d(1, 1, 0)
-            turn_d(1, 1, 1)
-            share(0, 0)
-            invert_a(0, 2, 2)
-            expo(1, 1, 0)
-            turn_d(1, 0, 0)
-            invert_c(0, 2)
-            turn_d(1, 2, 0)
-            expo(1, 1, 1)
-            turn_d(1, 0, 1)
-            result(0, 1, 2, "act")
-            fsum(1, 1, 0)
-            invert_e(0, 2, 2)
-            expo(1, 0, 0)
-            result(0, 0, 2, "act")
-            share(0, 2)
-            expo(1, 0, 1)
-            fsum(1, 0, 0)
-            share(0, 3)
-            invert_a(1, 0, 2)
-            expo(1, 2, 0)
-            turn_d(1, 2, 1)
-            result(0, 2, 2, "act")
-            expo(1, 2, 1)
-            turn_d(1, 3, 0)
-            turn_d(1, 3, 1)
-            fsum(1, 2, 2)
-            expo(1, 3, 0)
-            invert_c(1, 0)
-            result(0, 3, 2, "act")
-            expo(1, 3, 1)
-            fsum(1, 3, 2)
-            weave_y(0, 2, "act")
-            invert_e(1, 0, 2)
-            invert_a(1, 2, 2)
-            quant_y(0, 2)
-            share(1, 0)
+            mm2(2, 2)
+            leave(2, 2, "act")
+            leave(2, 6, "act")
+            leave(2, 3, "act")
+            low1(2, 2)
+            low1(2, 3)
+            low2(2, 2)
+            turn_d(2, 1)
+            invert_e(0)
+            low2(2, 3)
+            expo(2, 1)
+            turn_d(3, 0)
+            expo(3, 0)
+            turn_d(3, 1)
+            expo(3, 1)
+            fsum(3)
+            turn_d(2, 0)
+            expo(2, 0)
+            fsum(2)
+            share(1)
+            invert_a(1)
+            share(0)
+            invert_c(1)
+            heat(1, 13, "on")
+            low4(2, "act")
+            heat(1, 19, "on")
+            turn_d(7, 0)
+            expo(7, 0)
+            turn_d(7, 1)
+            expo(7, 1)
+            fsum(7)
+            invert_e(1)
+            result(1, 2, "act")
+            turn_d(6, 1)
+            turn_d(6, 0)
+            share(2)
+            result(0, 2, "act")
+            expo(6, 1)
+            expo(6, 0)
+            fsum(6)
+            share(3)
+            invert_a(3)
+            turn_d(5, 1)
+            expo(5, 1)
+            turn_d(5, 0)
+            expo(5, 0)
+            fsum(5)
+            heat(1, 14, "on")
+            invert_c(3)
+            result(2, 2, "act")
+            turn_d(4, 0)
+            expo(4, 0)
+            result(3, 2, "act")
+            turn_d(4, 1)
+            expo(4, 1)
+            fsum(4)
+            invert_e(3)
+            invert_a(2)
+            share(6)
             weave_y(0, 1, "act")
-            heat(1, 0, "on")
             quant_y(0, 1)
             weave_y(0, 0, "act")
-            share(1, 1)
-            invert_c(1, 2)
+            weave_y(0, 2, "act")
+            invert_c(2)
+            result(6, 1, "act")
             quant_y(0, 0)
-            heat(1, 18, "on")
+            invert_e(2)
+            quant_y(0, 2)
+            share(5)
             weave_y(0, 3, "act")
+            result(6, 0, "act")
             quant_y(0, 3)
-            heat(1, 12, "on")
-            heat(1, 21, "on")
-            result(1, 0, 2, "act")
-            invert_e(1, 2, 2)
-            result(1, 1, 2, "act")
-            share(1, 2)
-            result(1, 2, 0, "act")
-            share(1, 3)
-            heat(1, 15, "on")
-            result(1, 2, 1, "dve")
-            heat(1, 2, "on")
-            result(1, 3, 0, "dve")
+            result(5, 2, "act")
+            share(7)
+            result(7, 1, "act")
+            result(7, 0, "act")
+            share(4)
+            result(4, 2, "dve")
             weave_y(1, 1, "dve")
-            result(1, 3, 1, "act")
-            weave_y(1, 2, "dve")
-            weave_y(1, 0, "act")
-            weave_y(1, 3, "act")
             quant_y(1, 1)
+            weave_y(1, 0, "act")
+            weave_y(1, 2, "dve")
             quant_y(1, 2)
+            weave_y(1, 3, "act")
             quant_y(1, 0)
             quant_y(1, 3)
+            heat(1, 15, "on")

from contextlib import ExitStack

import concourse.mybir as mybir
from concourse.masks import make_identity

F32 = mybir.dt.float32
BF16 = mybir.dt.bfloat16
U32 = mybir.dt.uint32
I32 = mybir.dt.int32
U8 = mybir.dt.uint8
FP8X4 = mybir.dt.float8_e4m3fn_x4
FP4X4 = mybir.dt.float4_e2m1fn_x4
ALU = mybir.AluOpType
ACT = mybir.ActivationFunctionType

N = 1024
D = 1024
R = 8
P = 128
HALF = 512

FLOPS = 2 * 2 * N * D * D


def tile_bprexcessdelaylogitroutesplit_x2_kernel(
    tc, x, dlt_words, dlt_scales, f0, cap, t0, perc_words, perc_scales, c0, out_0, out_1, out_2
):
    nc = tc.nc
    with ExitStack() as ctx:
        keep = ctx.enter_context(tc.tile_pool(name="keep", bufs=1))
        two = ctx.enter_context(tc.tile_pool(name="two", bufs=2))
        five = ctx.enter_context(tc.tile_pool(name="five", bufs=5))
        four = ctx.enter_context(tc.tile_pool(name="four", bufs=4))
        three = ctx.enter_context(tc.tile_pool(name="three", bufs=3))
        turn = ctx.enter_context(tc.psum_pool(name="turn", bufs=3))
        spare = ctx.enter_context(tc.psum_pool(name="spare", bufs=1))
        mm = ctx.enter_context(tc.psum_pool(name="mm", bufs=4))

        x_rows = x.rearrange("(g m t) k -> g m t k", g=2, t=4)
        x_sb = [keep.tile([P, 4, D], BF16, name="x_sb%d" % g, align_bytes=64) for g in range(2)]
        raw, raw_s, vec = {}, {}, {}
        for key in ("dlt", "perc"):
            raw[key] = keep.tile([P, 2, 2 * D], U8, name="raw_" + key, align_bytes=64)
            raw_s[key] = keep.tile([P, 2, D], U8, name="raws_" + key, align_bytes=64)

        def load_words(key, src, h):
            cols = slice(256 * h, 256 * (h + 1))
            nc.sync.dma_start(
                out=raw[key][:].rearrange("p g b -> p (g b)").bitcast(I32).rearrange("p (g w) -> p g w", g=2)[:, :, cols],
                in_=src.bitcast(I32).rearrange("g p w -> p g w")[:, :, cols],
            )

        def load_scales(key, src, eng):
            for q in range(4):
                eng.dma_start(
                    out=raw_s[key][32 * q : 32 * q + 4, :, :].bitcast(I32),
                    in_=src[:, 4 * q : 4 * q + 4, :].bitcast(I32).rearrange("g q w -> q g w"),
                )

        ident = keep.tile([P, P], F32)
        make_identity(nc, ident[:])
        blank = keep.tile([P, HALF], BF16, align_bytes=64)
        nc.vector.memset(raw_s["dlt"][:].rearrange("p g n -> p (g n)").bitcast(I32), 0)
        nc.vector.memset(blank[:], 0.0)
        nc.vector.memset(raw_s["perc"][:].rearrange("p g n -> p (g n)").bitcast(I32), 0)
        load_words("dlt", dlt_words, 0)
        for tt in (0, 2):
            nc.sync.dma_start(out=x_sb[0][:, tt : tt + 2, :], in_=x_rows[0, :, tt : tt + 2, :])
            if tt == 0:
                load_words("dlt", dlt_words, 1)
        load_scales("dlt", dlt_scales, nc.scalar)
        for key, src in (("cap", cap), ("f0", f0), ("t0", t0)):
            vec[key] = keep.tile([P, 2, 4], BF16, name="v_" + key)
            nc.gpsimd.dma_start(out=vec[key][:], in_=src.rearrange("(h p t) -> p h t", h=2, t=4))
        c0_bf = keep.tile([P, R], BF16)
        nc.gpsimd.dma_start(out=c0_bf[:], in_=c0.rearrange("(o r) -> o r", r=R))
        load_scales("perc", perc_scales, nc.gpsimd)
        load_words("perc", perc_words, 0)
        load_words("perc", perc_words, 1)
        for tt in (0, 2):
            nc.sync.dma_start(out=x_sb[1][:, tt : tt + 2, :], in_=x_rows[1, :, tt : tt + 2, :])

        dw = keep.tile([P, 2, 2 * D], U8, align_bytes=64)
        ds = keep.tile([P, 2, D], U8, align_bytes=64)
        pw = keep.tile([P, 2, 2 * D], U8, align_bytes=64)
        psc = keep.tile([P, 2, D], U8, align_bytes=64)

        def perm_dlt(h):
            for g in range(2):
                nc.vector.tensor_copy(
                    out=dw[:, g, 1024 * h : 1024 * (h + 1)].rearrange("p (t m b) -> p t m b", t=4, b=2),
                    in_=raw["dlt"][:, g, 1024 * h : 1024 * (h + 1)].rearrange("p (m t b) -> p t m b", t=4, b=2),
                )

        def perm_dlt_scales(h):
            for g in range(2):
                nc.vector.tensor_copy(
                    out=ds[:, g, HALF * h : HALF * (h + 1)].rearrange("p (t m) -> p t m", t=4),
                    in_=raw_s["dlt"][:, g, HALF * h : HALF * (h + 1)].rearrange("p (m t) -> p t m", t=4),
                )

        def perm_perc_words(g):
            nc.vector.tensor_copy(
                out=pw[:, g, :].rearrange("p (r o b) -> p r o b", r=R, b=2),
                in_=raw["perc"][:, g, :].rearrange("p (o r b) -> p r o b", r=R, b=2),
            )

        def perm_perc_scales(g):
            nc.vector.tensor_copy(
                out=psc[:, g, :].rearrange("p (r o) -> p r o", r=R),
                in_=raw_s["perc"][:, g, :].rearrange("p (o r) -> p r o", r=R),
            )

        def flat(tile):
            return tile[:].rearrange("p h t -> p (h t)")

        inv_cap = keep.tile([P, 8], F32)
        base = keep.tile([P, 8], F32)
        base2 = keep.tile([P, 8], F32)
        base4 = keep.tile([P, 8], F32)
        gain = keep.tile([P, 8], F32)
        shift = keep.tile([P, 8], F32)
        c0_col = keep.tile([P, R], F32)

        def constants():
            nc.vector.reciprocal(inv_cap[:], flat(vec["cap"]))
            nc.vector.tensor_scalar(out=gain[:], in0=flat(vec["t0"]), scalar1=0.15, scalar2=None, op0=ALU.mult)
            nc.vector.tensor_tensor(out=base[:], in0=flat(vec["f0"]), in1=inv_cap[:], op=ALU.mult)
            nc.vector.tensor_copy(out=c0_col[:], in_=c0_bf[:])
            nc.vector.tensor_tensor(out=base2[:], in0=base[:], in1=base[:], op=ALU.mult)
            nc.vector.tensor_tensor(out=base4[:], in0=base2[:], in1=base2[:], op=ALU.mult)
            nc.vector.scalar_tensor_tensor(out=shift[:], in0=base4[:], scalar=-1.0, in1=gain[:], op0=ALU.mult, op1=ALU.mult)

        CH = [[0,1],[2,3],[4,5,6,7]]
        store = {}

        def get(key, pool, shape, dtype, name, **kw):
            if key not in store:
                store[key] = pool.tile(shape, dtype, name=name, **kw)
            return store[key]

        idle = spare.tile([P, HALF], F32, name="idle")

        def warm(n, k, eng):
            for _ in range(n if eng == "on" else 0):
                nc.tensor.matmul(idle[:], blank[:, 0:P], blank[:], start=True, stop=True)

        def heat(n, k, eng):
            for _ in range(n if eng == "on" else 0):
                nc.tensor.matmul_mx(
                    out=idle[:, 0 : width(HOT)],
                    lhsT=dw[:, 0, 0:256].bitcast(FP4X4),
                    lhsT_scale=ds[:, 0, 0:P],
                    rhs=store["xc", HOT][:, 0, :].bitcast(FP8X4),
                    rhs_scale=store["xs", HOT][:, 0, :],
                    start=True,
                    stop=True,
                )

        HOT = max(range(len(CH)), key=lambda c: (len(CH[c]), -c))

        def where(slot):
            for c, slots in enumerate(CH):
                if slot in slots:
                    return c, slots.index(slot)

        def width(c):
            return P * len(CH[c])

        def turn_x(slot):
            g, t = slot // 4, slot % 4
            words = x_sb[g][:].rearrange("p t k -> p (t k)").bitcast(F32)
            bk = get(("xt", slot), turn, [P, 4, P], F32, "bank")
            for k in range(2):
                for uu in range(2):
                    lo = HALF * t + 256 * k
                    nc.tensor.transpose(bk[:, 2 * k + uu, :], words[:, lo + uu : lo + 256 : 2], ident[:])

        def copy_x(slot, eng):
            c, i = where(slot)
            xg = get(("xg", c), two, [P, 2, width(c), 4], BF16, "xg", align_bytes=64)
            out = xg[:].rearrange("p k n j -> p (k n j)").bitcast(F32)
            out = out.rearrange("p (k n u) -> p k n u", k=2, u=2)[:, :, P * i : P * (i + 1), :]
            src = store["xt", slot][:].rearrange("p (k u) m -> p k m u", k=2)
            if eng == "act":
                nc.scalar.copy(out=out, in_=src)
            else:
                nc.vector.tensor_copy(out=out, in_=src)

        def quant_x(c, k):
            xc = get(("xc", c), two, [P, 2, width(c)], U32, "xc", align_bytes=64)
            xs = get(("xs", c), two, [P, 2, width(c)], U8, "xs", align_bytes=64)
            nc.vector.quantize_mx(
                out=xc[:, k, :].bitcast(FP8X4), scales=xs[:, k, :],
                in_=store["xg", c][:, k, :, :].rearrange("p n j -> p (n j)"),
            )

        def product(out, weight, wscale, col, codes, scales, cols):
            step = cols if cols == HALF else P
            for n in range(0, cols, step):
                for k in range(2):
                    nc.tensor.matmul_mx(
                        out=out[:, n : n + step],
                        lhsT=weight[:, k, 2 * col : 2 * (col + P)].bitcast(FP4X4),
                        lhsT_scale=wscale[:, k, col : col + P],
                        rhs=codes[:, k, n : n + step].bitcast(FP8X4),
                        rhs_scale=scales[:, k, n : n + step],
                        start=(k == 0),
                        stop=(k == 1),
                    )

        def mm1(c, h, i):
            v = HALF // width(c)
            a = get(("a1", c, h, i), mm, [P, v, width(c)], F32, "acc")
            for j in range(v):
                product(a[:, j, :], dw, ds, HALF * h + P * (v * i + j), store["xc", c], store["xs", c], width(c))

        def sq1(c, h, i):
            v = HALF // width(c)
            q = get(("q", c, h), two, [P, 4, width(c)], F32, "q")
            for j in range(v):
                t = v * i + j
                e = 4 * h + t
                nc.scalar.activation(
                    out=q[:, t, :], in_=store["a1", c, h, i][:, j, :], func=ACT.Square,
                    scale=inv_cap[:, e : e + 1], bias=base[:, e : e + 1],
                )

        def sq2(c, h, i, eng):
            v = store["q", c, h][:, 2 * i : 2 * i + 2, :]
            if eng == "act":
                nc.scalar.activation(out=v, in_=v, func=ACT.Square)
            else:
                nc.vector.tensor_tensor(out=v, in0=v, in1=v, op=ALU.mult)

        def affine(c, h, t, eng):
            e = 4 * h + t
            e16 = get(("e16", c, h), two, [P, 4, width(c)], BF16, "e16", align_bytes=64)
            src = store["q", c, h][:, t, :]
            if eng == "act":
                nc.scalar.activation(
                    out=e16[:, t, :], in_=src, func=ACT.Identity, scale=gain[:, e : e + 1], bias=shift[:, e : e + 1]
                )
            else:
                nc.vector.tensor_scalar(
                    out=e16[:, t, :], in0=src, scalar1=base4[:, e : e + 1], scalar2=gain[:, e : e + 1],
                    op0=ALU.subtract, op1=ALU.mult,
                )

        def weave_e(c, h, eng):
            eg = get(("eg", c, h), two, [P, width(c), 4], BF16, "eg", align_bytes=64)
            out = eg[:].rearrange("p (c i) t -> p c t i", i=4)
            src = store["e16", c, h][:].rearrange("p t (c i) -> p c t i", i=4)
            if eng == "act":
                nc.scalar.copy(out=out, in_=src)
            else:
                nc.vector.tensor_copy(out=out, in_=src)

        def quant_e(c, h):
            ec = get(("ec", c), two, [P, 2, width(c)], U32, "ec", align_bytes=64)
            es = get(("es", c), two, [P, 2, width(c)], U8, "es", align_bytes=64)
            nc.vector.quantize_mx(
                out=ec[:, h, :].bitcast(FP8X4), scales=es[:, h, :],
                in_=store["eg", c, h][:].rearrange("p n j -> p (n j)"),
            )

        def routes(c, i):
            return (i,) if width(c) == HALF else (i, i + 4)

        def mm2(c, i):
            rs = routes(c, i)
            a = get(("a2", c, i), mm, [P, len(rs), width(c)], F32, "acc")
            for j, r in enumerate(rs):
                product(a[:, j, :], pw, psc, P * r, store["ec", c], store["es", c], width(c))

        def leave(c, i, eng):
            cc = get(("cc", c), two, [P, R, width(c)], F32, "cc")
            for j, r in enumerate(routes(c, i)):
                if eng == "act":
                    nc.scalar.activation(
                        out=cc[:, r, :], in_=store["a2", c, i][:, j, :], func=ACT.Identity, scale=1.0,
                        bias=c0_col[:, r : r + 1],
                    )
                else:
                    nc.vector.tensor_scalar(
                        out=cc[:, r, :], in0=store["a2", c, i][:, j, :], scalar1=c0_col[:, r : r + 1], scalar2=None,
                        op0=ALU.add,
                    )

        def tmin(out, in0, in1):
            nc.vector.tensor_tensor(out=out, in0=in0, in1=in1, op=ALU.min)

        def low1(c, i):
            cc = store["cc", c]
            low = get(("low", c), keep, [P, 4, width(c)], F32, "low")
            v = HALF // width(c)
            tmin(low[:, v * i : v * (i + 1), :], cc[:, v * i : v * (i + 1), :], cc[:, v * i + 4 : v * (i + 1) + 4, :])

        def low2(c, i):
            low = store["low", c]
            negm = get(("negm", c), two, [P, width(c)], F32, "negm")
            if width(c) == HALF:
                tmin(low[:, i, :] if i < 3 else negm[:], low[:, i - 1, :], low[:, i, :])
            elif i == 1:
                tmin(low[:, 0:2, :], low[:, 0:2, :], low[:, 2:4, :])
            else:
                tmin(negm[:], low[:, 0, :], low[:, 1, :])

        def low4(c, eng):
            negm = store["negm", c]
            if eng == "act":
                nc.scalar.activation(out=negm[:], in_=negm[:], func=ACT.Copy, scale=-1.0)
            else:
                nc.vector.tensor_scalar(out=negm[:], in0=negm[:], scalar1=-1.0, scalar2=None, op0=ALU.mult)

        def turn_d(slot, hf):
            c, i = where(slot)
            cols = slice(P * i, P * (i + 1))
            cc, negm = store["cc", c], store["negm", c]
            b = get(("d", slot, hf), turn, [P, 4, P], F32, "bank")
            for j in range(4):
                nc.tensor.matmul(b[:, j, :], cc[:, 4 * hf + j, cols], ident[:], start=True, stop=False, is_transpose=True)
                nc.tensor.matmul(b[:, j, :], negm[:, cols], ident[:], start=False, stop=True, is_transpose=True)

        def expo(slot, hf):
            w = get(("w", slot), five, [P, P, R], F32, "w")
            nc.scalar.activation(
                out=w[:, :, 4 * hf : 4 * hf + 4], in_=store["d", slot, hf][:].rearrange("m r o -> m o r"),
                func=ACT.Exp, scale=-1.0,
            )

        def fsum(slot):
            tot = get(("tot", slot // 2), two, [P, 2, P], F32, "total_s")
            nc.vector.tensor_reduce(
                out=tot[:, slot % 2, :], in_=store["w", slot][:], axis=mybir.AxisListType.X, op=ALU.add
            )

        def mul(out, in0, in1):
            nc.vector.tensor_tensor(out=out, in0=in0, in1=in1, op=ALU.mult)

        def invert_a(p):
            prod = get(("prod", p), two, [P, P], F32, "prod")
            tot = store["tot", p]
            mul(prod[:], tot[:, 0, :], tot[:, 1, :])

        def invert_c(p):
            rec = get(("rec", p), two, [P, P], F32, "rec")
            nc.vector.reciprocal(rec[:], store["prod", p][:])

        def invert_e(p):
            inv = get(("inv", p), two, [P, 2, P], F32, "inv")
            tot = store["tot", p]
            mul(inv[:, 0, :], store["rec", p][:], tot[:, 1, :])
            mul(inv[:, 1, :], store["rec", p][:], tot[:, 0, :])

        def share(slot):
            w = store["w", slot]
            mul(w[:], w[:], store["inv", slot // 2][:, slot % 2, :].unsqueeze(2).to_broadcast([P, P, R]))

        def result(slot, part, eng):
            g, t = slot // 4, slot % 4
            y = get(("y", g), two, [P, 4, D], F32, "y")
            cols = (slice(0, HALF), slice(HALF, D), slice(0, D))[part]
            out = y[:, t, cols]
            src = store["w", slot][:].rearrange("m o r -> m (o r)")[:, cols]
            if eng == "act":
                nc.scalar.activation(out=out, in_=src, func=ACT.Copy, scale=8.0, bias=-1.0)
            else:
                nc.vector.tensor_scalar(out=out, in0=src, scalar1=8.0, scalar2=-1.0, op0=ALU.mult, op1=ALU.add)
            nc.sync.dma_start(
                out=out_0.rearrange("(g m t) p -> g m t p", g=2, t=4)[g, :, t, cols], in_=out
            )

        def weave_y(g, c, eng):
            if ("yw", g) not in store:
                get(("yw", g), two, [P, D], U32, "yw", align_bytes=64)
                ysc = get(("ysc", g), two, [P, D], U8, "ysc", align_bytes=64)
                nc.gpsimd.memset(ysc[:].bitcast(I32), 0)
            yb = get(("yb", g, c), four, [P, 256, 4], BF16, "yb", align_bytes=64)
            cols = slice(256 * c, 256 * (c + 1))
            out = yb[:].rearrange("p (c i) t -> p c t i", i=4)
            src = store["y", g][:, :, cols].rearrange("p t (c i) -> p c t i", i=4)
            if eng == "act":
                nc.scalar.copy(out=out, in_=src)
            else:
                nc.vector.tensor_copy(out=out, in_=src)

        def quant_y(g, c):
            yw, ysc = store["yw", g], store["ysc", g]
            cols = slice(256 * c, 256 * (c + 1))
            nc.vector.quantize_mx(
                out=yw[:, cols].bitcast(FP8X4), scales=ysc[:, cols],
                in_=store["yb", g, c][:].rearrange("p n j -> p (n j)"),
            )
            nc.sync.dma_start(
                out=out_1[g].rearrange("m p t -> m (p t)").bitcast(I32)[:, cols], in_=yw[:, cols].bitcast(I32)
            )
            store["done", g] = store.get(("done", g), 0) + 1
            if store["done", g] == 4:
                for qd in range(4):
                    nc.sync.dma_start(
                        out=out_2[g, 4 * qd : 4 * qd + 4, :].bitcast(I32),
                        in_=ysc[32 * qd : 32 * qd + 4, :].bitcast(I32),
                    )


        with tc.manual_schedule():
            warm(6, 0, "on")
            perm_dlt(0)
            perm_dlt_scales(0)
            perm_dlt_scales(1)
            turn_x(0)
            turn_x(1)
            copy_x(0, "act")
            turn_x(2)
            constants()
            copy_x(1, "act")
            quant_x(0, 0)
            turn_x(3)
            copy_x(2, "act")
            quant_x(0, 1)
            perm_perc_words(1)
            perm_dlt(1)
            copy_x(3, "act")
            quant_x(1, 1)
            mm1(0, 0, 1)
            perm_perc_scales(1)
            perm_perc_scales(0)
            sq1(0, 0, 1)
            sq2(0, 0, 1, "act")
            perm_perc_words(0)
            affine(0, 0, 3, "dve")
            quant_x(1, 0)
            affine(0, 0, 2, "dve")
            mm1(0, 0, 0)
            sq1(0, 0, 0)
            turn_x(4)
            turn_x(6)
            mm1(0, 1, 1)
            copy_x(6, "dve")
            copy_x(4, "act")
            sq2(0, 0, 0, "act")
            mm1(0, 1, 0)
            sq1(0, 1, 1)
            sq2(0, 1, 1, "dve")
            sq1(0, 1, 0)
            sq2(0, 1, 0, "dve")
            affine(0, 1, 2, "dve")
            affine(0, 1, 3, "dve")
            turn_x(7)
            affine(0, 1, 0, "dve")
            affine(0, 0, 1, "act")
            affine(0, 0, 0, "act")
            weave_e(0, 0, "dve")
            copy_x(7, "dve")
            turn_x(5)
            copy_x(5, "act")
            affine(0, 1, 1, "act")
            mm1(1, 1, 0)
            mm1(1, 0, 1)
            sq1(1, 1, 0)
            sq1(1, 0, 1)
            weave_e(0, 1, "dve")
            quant_e(0, 0)
            quant_e(0, 1)
            quant_x(2, 0)
            quant_x(2, 1)
            sq2(1, 0, 1, "dve")
            mm1(1, 1, 1)
            sq1(1, 1, 1)
            sq2(1, 1, 0, "act")
            affine(1, 1, 1, "dve")
            mm1(1, 0, 0)
            sq2(1, 1, 1, "act")
            sq1(1, 0, 0)
            affine(1, 1, 2, "act")
            affine(1, 1, 0, "act")
            mm2(0, 3)
            sq2(1, 0, 0, "dve")
            leave(0, 3, "act")
            mm2(0, 2)
            leave(0, 2, "act")
            affine(1, 0, 2, "dve")
            affine(1, 1, 3, "dve")
            affine(1, 0, 3, "dve")
            affine(1, 0, 0, "dve")
            weave_e(1, 1, "dve")
            low1(0, 1)
            mm1(2, 0, 2)
            mm1(2, 0, 3)
            affine(1, 0, 1, "act")
            mm2(0, 0)
            mm2(0, 1)
            sq1(2, 0, 3)
            sq1(2, 0, 2)
            leave(0, 0, "act")
            leave(0, 1, "act")
            quant_e(1, 1)
            mm1(2, 0, 0)
            sq1(2, 0, 0)
            sq2(2, 0, 1, "dve")
            low1(0, 0)
            weave_e(1, 0, "dve")
            affine(2, 0, 2, "dve")
            mm1(2, 0, 1)
            sq1(2, 0, 1)
            low2(0, 1)
            sq2(2, 0, 0, "dve")
            quant_e(1, 0)
            affine(2, 0, 3, "dve")
            affine(2, 0, 0, "dve")
            low2(0, 2)
            affine(2, 0, 1, "dve")
            mm1(2, 1, 3)
            sq1(2, 1, 3)
            mm1(2, 1, 2)
            sq1(2, 1, 2)
            mm1(2, 1, 0)
            sq1(2, 1, 0)
            mm1(2, 1, 1)
            sq1(2, 1, 1)
            sq2(2, 1, 1, "act")
            sq2(2, 1, 0, "act")
            low4(0, "act")
            mm2(1, 2)
            affine(2, 1, 3, "dve")
            weave_e(2, 0, "dve")
            leave(1, 2, "dve")
            affine(2, 1, 1, "act")
            affine(2, 1, 0, "act")
            affine(2, 1, 2, "act")
            mm2(1, 0)
            quant_e(2, 0)
            turn_d(0, 1)
            mm2(1, 1)
            weave_e(2, 1, "dve")
            leave(1, 0, "act")
            leave(1, 1, "act")
            low1(1, 0)
            quant_e(2, 1)
            turn_d(1, 0)
            mm2(1, 3)
            expo(0, 1)
            leave(1, 3, "act")
            low1(1, 1)
            turn_d(0, 0)
            turn_d(1, 1)
            expo(0, 0)
            fsum(0)
            mm2(2, 5)
            expo(1, 0)
            low2(1, 1)
            expo(1, 1)
            fsum(1)
            mm2(2, 1)
            leave(2, 5, "act")
            low2(1, 2)
            leave(2, 1, "act")
            mm2(2, 0)
            invert_a(0)
            mm2(2, 4)
            low1(2, 1)
            leave(2, 0, "act")
            leave(2, 4, "act")
            low1(2, 0)
            invert_c(0)
            low2(2, 1)
            mm2(2, 3)
            mm2(2, 7)
            leave(2, 7, "act")
            mm2(2, 6)
            low4(1, "act")
            mm2(2, 2)
            leave(2, 2, "act")
            leave(2, 6, "act")
            leave(2, 3, "act")
            low1(2, 2)
            low1(2, 3)
            low2(2, 2)
            turn_d(2, 1)
            invert_e(0)
            low2(2, 3)
            expo(2, 1)
            turn_d(3, 0)
            expo(3, 0)
            turn_d(3, 1)
            expo(3, 1)
            fsum(3)
            turn_d(2, 0)
            expo(2, 0)
            fsum(2)
            share(1)
            invert_a(1)
            share(0)
            invert_c(1)
            heat(1, 13, "on")
            low4(2, "act")
            heat(1, 19, "on")
            turn_d(7, 0)
            expo(7, 0)
            turn_d(7, 1)
            expo(7, 1)
            fsum(7)
            invert_e(1)
            result(1, 2, "act")
            turn_d(6, 1)
            turn_d(6, 0)
            share(2)
            result(0, 2, "act")
            expo(6, 1)
            expo(6, 0)
            fsum(6)
            share(3)
            invert_a(3)
            turn_d(5, 1)
            expo(5, 1)
            turn_d(5, 0)
            expo(5, 0)
            fsum(5)
            heat(1, 14, "on")
            invert_c(3)
            result(2, 2, "act")
            turn_d(4, 0)
            expo(4, 0)
            result(3, 2, "act")
            turn_d(4, 1)
            expo(4, 1)
            fsum(4)
            invert_e(3)
            invert_a(2)
            share(6)
            weave_y(0, 1, "act")
            quant_y(0, 1)
            weave_y(0, 0, "act")
            weave_y(0, 2, "act")
            invert_c(2)
            result(6, 1, "act")
            quant_y(0, 0)
            invert_e(2)
            quant_y(0, 2)
            share(5)
            weave_y(0, 3, "act")
            result(6, 0, "act")
            quant_y(0, 3)
            result(5, 2, "act")
            share(7)
            result(7, 1, "act")
            result(7, 0, "act")
            share(4)
            result(4, 2, "dve")
            weave_y(1, 1, "dve")
            quant_y(1, 1)
            weave_y(1, 0, "act")
            weave_y(1, 2, "dve")
            quant_y(1, 2)
            weave_y(1, 3, "act")
            quant_y(1, 0)
            quant_y(1, 3)
            heat(1, 15, "on")
